import numpy as np
import ml_dtypes


def mxq(x, axis, fmt="e4m3"):
    dtype, down = {"e4m3": (ml_dtypes.float8_e4m3fn, 7), "e5m2": (ml_dtypes.float8_e5m2, 14)}[fmt]
    v = np.moveaxis(np.asarray(x, np.float32).astype(ml_dtypes.bfloat16).astype(np.float64), axis, -1)
    blocks = v.reshape(v.shape[:-1] + (-1, 32))
    amax = np.abs(blocks).max(-1, keepdims=True)
    byte = np.maximum(np.where(amax > 0, np.frexp(amax)[1] - 1 + 127, 0) - down, 1)
    scale = np.exp2(byte - 127.0)
    codes = (blocks / scale).astype(np.float32).astype(dtype).astype(np.float64)
    return np.moveaxis((codes * scale).reshape(v.shape), -1, axis)


WIDE = False


def mx_kscale(k):
    if not WIDE:
        return np.ones(k)
    levels = np.array([10, -10, 5, -5, 0])
    if k % 512:
        return np.exp2(np.random.permutation(np.resize(levels, k // 32))).repeat(32)
    a = np.empty((k // 512, 16))
    for p in range(k // 512):
        a[p, :8] = np.random.permutation(np.resize(levels, 8))
        for g in range(8):
            far = levels[np.abs(levels - a[p, g]) >= 10]
            a[p, g + 8] = far[np.random.randint(len(far))]
    return np.exp2(a.ravel()).repeat(32)


def f64(x):
    return np.asarray(x).astype(np.float64)


def striped(idx):
    return np.tile(idx.reshape(-1, 16).T, (8, 1)).astype(np.uint16)


def unstriped(offs):
    return offs[:16].T.reshape(-1).astype(np.int64)


E2M1 = np.array([0.0, 0.5, 1.0, 1.5, 2.0, 3.0, 4.0, 6.0, -0.0, -0.5, -1.0, -1.5, -2.0, -3.0, -4.0, -6.0])


def pack_weight(w, fmt):
    k, n = w.shape
    w = f64(np.asarray(w, np.float32).astype(ml_dtypes.bfloat16)).reshape(k // 32, 32, n)
    amax = np.abs(w).max(1)
    if fmt == "e4m3":
        byte = np.frexp(amax)[1] - 1 + 127 - 7
    else:
        mant, ex = np.frexp(amax / 6.0)
        byte = np.where(mant > 0.5, ex, ex - 1) + 127
    byte = np.clip(np.where(amax > 0, byte, 1), 1, 254)
    scaled = (w * np.exp2(127.0 - byte)[:, None, :]).reshape(k, n).astype(np.float32)
    by_word = np.ascontiguousarray(scaled.reshape(k // 512, 128, 4, n).transpose(0, 1, 3, 2))
    if fmt == "e4m3":
        words = by_word.astype(ml_dtypes.float8_e4m3fn).view(np.uint8)
    else:
        c = by_word.astype(ml_dtypes.float4_e2m1fn).view(np.uint8) & 0xF
        words = (c[..., 0::2] | (c[..., 1::2] << 4)).reshape(k // 512, 128, 2 * n)
    return np.ascontiguousarray(words), np.ascontiguousarray(byte.astype(np.uint8).reshape(k // 512, 16, n))


def unpack_weight(words, scales, fmt):
    g, _, n = scales.shape
    words = np.ascontiguousarray(words).reshape(g, 128, n, -1)
    if fmt == "e4m3":
        vals = words.view(ml_dtypes.float8_e4m3fn).astype(np.float64)
    else:
        nib = np.empty((g, 128, n, 4), np.uint8)
        nib[..., 0::2] = words & 0xF
        nib[..., 1::2] = words >> 4
        vals = E2M1[nib]
    vals = vals * np.repeat(np.exp2(scales.astype(np.float64) - 127.0), 8, axis=1)[..., None]
    return vals.transpose(0, 1, 3, 2).reshape(g * 512, n)


def gelu(v):
    return 0.5 * v * (1.0 + np.tanh(np.sqrt(2.0 / np.pi) * (v + 0.044715 * v**3)))


def pack_table4(v):
    words, scales = pack_weight(v, "e2m1")
    g, t = words.shape[0] // 2, v.shape[1]
    words = words.reshape(g, 2, 128, t, 2).transpose(0, 2, 3, 1, 4)
    return np.concatenate([words.reshape(g, -1), scales.reshape(g, -1)], axis=1)


def unpack_table4(tab):
    g, t = tab.shape[0], tab.shape[1] // 544
    words = tab[:, :512 * t].reshape(g, 128, t, 2, 2).transpose(0, 3, 1, 2, 4).reshape(2 * g, 128, 2 * t)
    return unpack_weight(words, tab[:, 512 * t:].reshape(2 * g, 16, t), "e2m1")


K, T, S, H, N = 1024, 4096, 1024, 1024, 512

def setup_inputs():
    n = np.random.standard_normal
    s = mx_kscale(K)[:, None]
    u = mx_kscale(H)[:, None]
    tab = pack_table4(n((K, T)) * s)
    w1_words, w1_scales = pack_weight(n((K, H)) / np.sqrt(K) / s, "e2m1")
    gain = np.exp(0.3 * n(H)) * u[:, 0]
    wa = 1.5 * n((H, N)) / np.sqrt(H) / u
    wb = 1.5 * n((H, N)) / np.sqrt(H) / u
    return {
        "tab": tab,
        "offs": striped(np.random.permutation(T)[:S]),
        "w1_words": w1_words,
        "w1_scales": w1_scales,
        "gain": gain.astype(np.float32),
        "wa": wa.astype(np.float32),
        "ba": (0.5 * n(N)).astype(np.float32),
        "wb": wb.astype(np.float32),
        "bb": (0.5 * n(N)).astype(np.float32),
    }

def reference(tab, offs, w1_words, w1_scales, gain, wa, ba, wb, bb):
    v = unpack_table4(tab)[:, unstriped(offs)]
    w1 = unpack_weight(w1_words, w1_scales, "e2m1")
    h = np.tanh(w1.T @ v) * f64(gain)[:, None]
    hq = mxq(h, 0, "e4m3")
    qa = (mxq(f64(wa), 0, "e4m3").T @ hq) + f64(ba)[:, None]
    qb = (mxq(f64(wb), 0, "e4m3").T @ hq) + f64(bb)[:, None]
    return np.minimum(qa, qb)

@@ -1,0 +1,256 @@
+from contextlib import ExitStack
+
+import concourse.mybir as mybir
+from concourse.masks import make_identity
+
+K, T, S, H, N = 1024, 4096, 1024, 1024, 512
+FLOPS = 2 * K * H * S + 2 * 2 * H * N * S
+
+F32 = mybir.dt.float32
+BF16 = mybir.dt.bfloat16
+I32 = mybir.dt.int32
+U32 = mybir.dt.uint32
+U16 = mybir.dt.uint16
+U8 = mybir.dt.uint8
+FP8X4 = mybir.dt.float8_e4m3fn_x4
+FP4X4 = mybir.dt.float4_e2m1fn_x4
+ACT = mybir.ActivationFunctionType
+ALU = mybir.AluOpType
+
+P = 128
+HALF = 512
+QUART = 256
+
+
+def tile_list_replay_twin_critics_kernel(tc, tab, offs, w1_words, w1_scales, gain, wa, ba, wb, bb, out):
+    nc = tc.nc
+    with ExitStack() as ctx:
+        keep = ctx.enter_context(tc.tile_pool(name="keep", bufs=1))
+        ring = ctx.enter_context(tc.tile_pool(name="ring", bufs=3))
+        psum = ctx.enter_context(tc.psum_pool(name="psum", bufs=2))
+
+        offsets = keep.tile([P, S // 16], U16, name="offsets")
+        nc.sync.dma_start(offsets[:], offs)
+
+        tab_scales = keep.tile([P, T], U8, name="tab_scales", align_bytes=64)
+        w1s_raw = keep.tile([P, H], U8, name="w1s_raw", align_bytes=64)
+        nc.sync.dma_start(
+            tab_scales[0:32, :].bitcast(I32),
+            tab[0:1, 512 * T :].rearrange("o (a g t) -> (o g) a t", a=2, g=16).bitcast(I32),
+        )
+        nc.sync.dma_start(w1s_raw[0:32, :].bitcast(I32), w1_scales.rearrange("a g c -> g a c").bitcast(I32))
+        w1_raw = keep.tile([P, 2 * H // 2], I32, name="w1_raw", align_bytes=64)
+        nc.sync.dma_start(w1_raw[:].rearrange("p (a x) -> p a x", a=2), w1_words.rearrange("a p x -> p a x").bitcast(I32))
+        tab_words = keep.tile([P, T], I32, name="tab_words", align_bytes=64)
+        nc.sync.dma_start(tab_words[:], tab[0:1, 0 : 512 * T].rearrange("o (p x) -> (o p) x", p=P).bitcast(I32))
+
+        gain_t = keep.tile([P, 8], F32, name="gain_t")
+        nc.scalar.dma_start(gain_t[:].rearrange("p (b t) -> p b t", b=2), gain.rearrange("(b p t) -> p b t", b=2, t=4))
+
+        bias_rows = keep.tile([P, P], F32, name="bias_rows")
+        nc.vector.memset(bias_rows[:], 0.0)
+        for lo, hi in ((32, 64), (64, P)):
+            nc.vector.memset(w1s_raw[lo:hi, :].bitcast(I32), 0)
+            nc.vector.memset(tab_scales[lo:hi, :].bitcast(I32), 0)
+        planes = keep.tile([P, 2 * (S + H)], U8, name="planes", align_bytes=64)
+        nc.vector.memset(planes[:].bitcast(I32), 0)
+        nc.scalar.dma_start(bias_rows[0:4, :], ba.rearrange("(m p) -> m p", p=P))
+        nc.scalar.dma_start(bias_rows[4:8, :], bb.rearrange("(m p) -> m p", p=P))
+        ident = keep.tile([P, P], F32, name="ident")
+        make_identity(nc, ident[:])
+        warm_out = keep.tile([P, 8], F32, name="warm_out")
+        nc.scalar.activation(warm_out[:], ident[:, 0:8], ACT.Tanh)
+        bias_bank = psum.tile([P, P], F32, name="critic0")
+        nc.tensor.transpose(bias_bank[:], bias_rows[:], ident[:])
+        biases = keep.tile([P, 8], F32, name="biases")
+        nc.scalar.copy(biases[:], bias_bank[:, 0:8])
+
+        spread = keep.tile([P, S + H], U8, name="spread", align_bytes=64)
+        nc.vector.tensor_copy(
+            spread[:, S:].rearrange("p (b t o i) -> p b o t i", b=2, t=4, i=16),
+            w1s_raw[:].rearrange("p (b o i t) -> p b o t i", b=2, t=4, i=16),
+        )
+        picked_scales = keep.tile([P, S], U8, name="picked_scales", tag="late", align_bytes=64)
+        nc.vector.tensor_copy(picked_scales[:], tab_scales[:].indirect(offsets[:]))
+        nc.vector.tensor_copy(spread[:, 0:S].bitcast(I32), picked_scales[:].bitcast(I32))
+        for g in range(4):
+            nc.sync.dma_start(
+                planes[32 * g : 32 * g + 4, :].bitcast(I32).rearrange("p (a x) -> p a x", a=2),
+                spread[8 * g : 8 * g + 8, :].bitcast(I32),
+            )
+        w1_dealt = keep.tile([P, 2 * 2 * H], U8, name="w1_dealt", align_bytes=64)
+        nc.vector.tensor_copy(
+            w1_dealt[:].bitcast(U16).rearrange("p (c t o i) -> p c o t i", c=4, t=4, i=8),
+            w1_raw[:].bitcast(U16).rearrange("p (c o i t) -> p c o t i", c=4, t=4, i=8),
+        )
+
+        w_all = keep.tile([P, 4 * 4 * N], F32, name="w_all", tag="late", align_bytes=64)
+        w_raw = {}
+        for c, w in enumerate((wa, wb)):
+            for b in range(2):
+                w_raw[c, b] = w_all[:, (2 * c + b) * 4 * N : (2 * c + b + 1) * 4 * N]
+                nc.sync.dma_start(w_raw[c, b], w[512 * b : 512 * b + 512, :].rearrange("(p j) n -> p (j n)", j=4))
+
+        states = []
+        for s in range(2):
+            picked = keep.tile([P, HALF], U32, name=f"picked{s}", align_bytes=64)
+            nc.vector.tensor_copy(picked[:], tab_words[:].bitcast(U32).indirect(offsets[:, 32 * s : 32 * s + 32]))
+            parted = keep.tile([P, 2 * 2 * HALF], U8, name=f"parted{s}", align_bytes=64)
+            nc.vector.tensor_copy(
+                parted[:].bitcast(U16).rearrange("p (a o i) -> p o a i", a=2, i=8),
+                picked[:].bitcast(U16).rearrange("p (o i a) -> p o a i", a=2, i=8),
+            )
+            states.append(parted)
+
+        w_grouped = {}
+        w_codes = {}
+        w_planes = {}
+        for c in range(2):
+            for b in range(2):
+                w_grouped[c, b] = keep.tile([P, 4 * N], BF16, name=f"w_grouped{c}{b}", align_bytes=64)
+                w_codes[c, b] = keep.tile([P, N], U32, name=f"w_codes{c}{b}", align_bytes=64)
+                w_planes[c, b] = keep.tile([P, N], U8, name=f"w_planes{c}{b}", align_bytes=64)
+        h_codes = [keep.tile([P, S], U32, name=f"h_codes{b}", align_bytes=64) for b in range(2)]
+        h_planes = [keep.tile([P, S], U8, name=f"h_planes{b}", align_bytes=64) for b in range(2)]
+
+        def weave(c, b, half, on_vector):
+            cols = slice(half * 64, half * 64 + 64)
+            dst = w_grouped[c, b][:].rearrange("p (o i j) -> p o j i", i=4, j=4)[:, cols]
+            src = w_raw[c, b].rearrange("p (j o i) -> p o j i", i=4, j=4)[:, cols]
+            if on_vector:
+                nc.vector.tensor_copy(dst, src)
+            else:
+                nc.scalar.copy(dst, src)
+
+        def quantise_w(c, b):
+            nc.vector.quantize_mx(out=w_codes[c, b][:].bitcast(FP8X4), scales=w_planes[c, b][:], in_=w_grouped[c, b][:])
+
+        tanh_tiles = {}
+        h_grouped = {}
+
+        def encode(q, b):
+            s, j0 = divmod(q * QUART, HALF)
+            tanh_t = ring.tile([P, 2, QUART, 2], F32, name="tanh_t", align_bytes=64)
+            for u in range(2):
+                bank = psum.tile([P, 2, QUART], F32, name=f"enc{u}")
+                for v in range(2):
+                    t = 2 * u + v
+                    for a in range(2):
+                        col = a * H + b * 512 + t * P
+                        pcol = a * (S + H)
+                        nc.tensor.matmul_mx(
+                            out=bank[:, v, :],
+                            lhsT=w1_dealt[:, 2 * col : 2 * col + 2 * P].bitcast(FP4X4),
+                            lhsT_scale=planes[:, pcol + S + b * 512 + t * P : pcol + S + b * 512 + (t + 1) * P],
+                            rhs=states[s][:, 2 * (a * HALF + j0) : 2 * (a * HALF + j0 + QUART)].bitcast(FP4X4),
+                            rhs_scale=planes[:, pcol + q * QUART : pcol + (q + 1) * QUART],
+                            start=(a == 0),
+                            stop=(a == 1),
+                        )
+                nc.scalar.activation(tanh_t[:, u], bank[:].rearrange("p v n -> p n v"), ACT.Tanh)
+            tanh_tiles[q, b] = tanh_t
+
+        def apply_gain(q, b):
+            grouped = ring.tile([P, QUART * 4], BF16, name="h_grouped", align_bytes=64)
+            nc.vector.tensor_tensor(
+                grouped[:].rearrange("p (n u v) -> p n u v", u=2, v=2),
+                tanh_tiles[q, b][:].rearrange("p u n v -> p n u v"),
+                gain_t[:, 4 * b : 4 * b + 4].rearrange("p (o u v) -> p o u v", o=1, u=2).to_broadcast([P, QUART, 2, 2]),
+                ALU.mult,
+            )
+            h_grouped[q, b] = grouped
+
+        def quantise_h(q, b):
+            cols = slice(q * QUART, (q + 1) * QUART)
+            nc.vector.quantize_mx(out=h_codes[b][:, cols].bitcast(FP8X4), scales=h_planes[b][:, cols], in_=h_grouped[q, b][:])
+
+        def critic_bank(c, j0, width, m0):
+            per_bank = 512 // width
+            bank = psum.tile([P, per_bank, width], F32, name=f"critic{c}")
+            for i in range(per_bank):
+                rows = slice((m0 + i) * P, (m0 + i + 1) * P)
+                for b in range(2):
+                    nc.tensor.matmul_mx(
+                        out=bank[:, i, :],
+                        lhsT=w_codes[c, b][:, rows].bitcast(FP8X4),
+                        lhsT_scale=w_planes[c, b][:, rows],
+                        rhs=h_codes[b][:, j0 : j0 + width].bitcast(FP8X4),
+                        rhs_scale=h_planes[b][:, j0 : j0 + width],
+                        start=(b == 0),
+                        stop=(b == 1),
+                    )
+            return bank
+
+        qa_tiles = {}
+
+        def critic_a(j0, width, m0):
+            bank = critic_bank(0, j0, width, m0)
+            per_bank = 512 // width
+            qa = keep.tile([P, per_bank, width], F32, name=f"qa{j0}_{m0}")
+            for i in range(per_bank):
+                nc.scalar.activation(qa[:, i, :], bank[:, i, :], ACT.Identity, bias=biases[:, m0 + i : m0 + i + 1])
+            qa_tiles[j0, m0] = qa
+
+        def critic_b(j0, width, m0):
+            bank = critic_bank(1, j0, width, m0)
+            per_bank = 512 // width
+            res = keep.tile([P, per_bank, width], F32, name=f"res{j0}_{m0}")
+            for i in range(per_bank):
+                nc.vector.scalar_tensor_tensor(
+                    res[:, i, :], bank[:, i, :], biases[:, 4 + m0 + i : 4 + m0 + i + 1], qa_tiles[j0, m0][:, i, :], ALU.add, ALU.min
+                )
+            dst = out.rearrange("(m p) j -> p m j", p=P)[:, m0 : m0 + per_bank, j0 : j0 + width]
+            nc.sync.dma_start(dst, res[:])
+
+        encode(0, 0)
+        weave(0, 0, 0, True)
+        weave(0, 0, 1, True)
+        encode(0, 1)
+        apply_gain(0, 0)
+        quantise_w(0, 0)
+        weave(0, 1, 0, False)
+        apply_gain(0, 1)
+        quantise_h(0, 0)
+        weave(0, 1, 1, False)
+        encode(1, 0)
+        quantise_h(0, 1)
+        quantise_w(0, 1)
+        weave(1, 0, 0, False)
+        apply_gain(1, 0)
+        encode(1, 1)
+        weave(1, 0, 1, False)
+        weave(1, 1, 0, True)
+        quantise_h(1, 0)
+        apply_gain(1, 1)
+        quantise_w(1, 0)
+        weave(1, 1, 1, False)
+        quantise_h(1, 1)
+        encode(2, 0)
+        quantise_w(1, 1)
+        critic_a(0, 512, 0)
+        critic_b(0, 512, 0)
+        apply_gain(2, 0)
+        encode(2, 1)
+        critic_a(0, 512, 1)
+        critic_b(0, 512, 1)
+        quantise_h(2, 0)
+        apply_gain(2, 1)
+        encode(3, 0)
+        critic_a(0, 512, 2)
+        critic_b(0, 512, 2)
+        quantise_h(2, 1)
+        apply_gain(3, 0)
+        encode(3, 1)
+        critic_a(0, 512, 3)
+        critic_b(0, 512, 3)
+        quantise_h(3, 0)
+        apply_gain(3, 1)
+        critic_a(512, 256, 0)
+        critic_b(512, 256, 0)
+        quantise_h(3, 1)
+        critic_a(512, 256, 2)
+        critic_b(512, 256, 2)
+        critic_a(768, 256, 0)
+        critic_b(768, 256, 0)
+        critic_a(768, 256, 2)
+        critic_b(768, 256, 2)

@@ -20,6 +20,7 @@ ALU = mybir.AluOpType
 P = 128
 HALF = 512
 QUART = 256
+GPSIMD_TOKENS = (80, 112)
 
 
 def tile_list_replay_twin_critics_kernel(tc, tab, offs, w1_words, w1_scales, gain, wa, ba, wb, bb, out):
@@ -35,33 +36,35 @@ def tile_list_replay_twin_critics_kernel(tc, tab, offs, w1_words, w1_scales, gai
         tab_scales = keep.tile([P, T], U8, name="tab_scales", align_bytes=64)
         w1s_raw = keep.tile([P, H], U8, name="w1s_raw", align_bytes=64)
         nc.sync.dma_start(
-            tab_scales[0:32, :].bitcast(I32),
+            tab_scales[96:P, :].bitcast(I32),
             tab[0:1, 512 * T :].rearrange("o (a g t) -> (o g) a t", a=2, g=16).bitcast(I32),
         )
-        nc.sync.dma_start(w1s_raw[0:32, :].bitcast(I32), w1_scales.rearrange("a g c -> g a c").bitcast(I32))
-        w1_raw = keep.tile([P, 2 * H // 2], I32, name="w1_raw", align_bytes=64)
-        nc.sync.dma_start(w1_raw[:].rearrange("p (a x) -> p a x", a=2), w1_words.rearrange("a p x -> p a x").bitcast(I32))
+        nc.sync.dma_start(w1s_raw[96:P, :].bitcast(I32), w1_scales.rearrange("a g c -> g a c").bitcast(I32))
         tab_words = keep.tile([P, T], I32, name="tab_words", align_bytes=64)
         nc.sync.dma_start(tab_words[:], tab[0:1, 0 : 512 * T].rearrange("o (p x) -> (o p) x", p=P).bitcast(I32))
+        w1_raw = keep.tile([P, 2 * H // 2], I32, name="w1_raw", align_bytes=64)
+        nc.sync.dma_start(w1_raw[:].rearrange("p (a x) -> p a x", a=2), w1_words.rearrange("a p x -> p a x").bitcast(I32))
 
-        gain_t = keep.tile([P, 8], F32, name="gain_t")
-        nc.scalar.dma_start(gain_t[:].rearrange("p (b t) -> p b t", b=2), gain.rearrange("(b p t) -> p b t", b=2, t=4))
-
-        bias_rows = keep.tile([P, P], F32, name="bias_rows")
-        nc.vector.memset(bias_rows[:], 0.0)
-        for lo, hi in ((32, 64), (64, P)):
-            nc.vector.memset(w1s_raw[lo:hi, :].bitcast(I32), 0)
-            nc.vector.memset(tab_scales[lo:hi, :].bitcast(I32), 0)
+        nc.vector.memset(w1s_raw[0:96, :].bitcast(I32), 0)
+        nc.vector.memset(tab_scales[0:96, :].bitcast(I32), 0)
+        rows = keep.tile([P, 512 + P], F32, name="rows")
+        nc.vector.memset(rows[:], 0.0)
         planes = keep.tile([P, 2 * (S + H)], U8, name="planes", align_bytes=64)
         nc.vector.memset(planes[:].bitcast(I32), 0)
-        nc.scalar.dma_start(bias_rows[0:4, :], ba.rearrange("(m p) -> m p", p=P))
-        nc.scalar.dma_start(bias_rows[4:8, :], bb.rearrange("(m p) -> m p", p=P))
+        nc.scalar.dma_start(rows[0:2, 0:512], gain.rearrange("(b x) -> b x", b=2))
+        nc.gpsimd.dma_start(rows[0:4, 512:], ba.rearrange("(m p) -> m p", p=P))
+        nc.gpsimd.dma_start(rows[4:8, 512:], bb.rearrange("(m p) -> m p", p=P))
         ident = keep.tile([P, P], F32, name="ident")
         make_identity(nc, ident[:])
         warm_out = keep.tile([P, 8], F32, name="warm_out")
         nc.scalar.activation(warm_out[:], ident[:, 0:8], ACT.Tanh)
+        gain_bank = psum.tile([P, 4, P], F32, name="gain_bank", bufs=1)
+        for t in range(4):
+            nc.tensor.transpose(gain_bank[:, t, :], rows[:, t:512:4], ident[:])
+        gain_t = keep.tile([P, 2, 4], F32, name="gain_t")
+        nc.scalar.copy(gain_t[:], gain_bank[:, :, 0:2].rearrange("p t b -> p b t"))
         bias_bank = psum.tile([P, P], F32, name="critic0")
-        nc.tensor.transpose(bias_bank[:], bias_rows[:], ident[:])
+        nc.tensor.transpose(bias_bank[:], rows[:, 512:], ident[:])
         biases = keep.tile([P, 8], F32, name="biases")
         nc.scalar.copy(biases[:], bias_bank[:, 0:8])
 
@@ -76,24 +79,34 @@ def tile_list_replay_twin_critics_kernel(tc, tab, offs, w1_words, w1_scales, gai
         for g in range(4):
             nc.sync.dma_start(
                 planes[32 * g : 32 * g + 4, :].bitcast(I32).rearrange("p (a x) -> p a x", a=2),
-                spread[8 * g : 8 * g + 8, :].bitcast(I32),
+                spread[96 + 8 * g : 96 + 8 * g + 8, :].bitcast(I32),
             )
-        w1_dealt = keep.tile([P, 2 * 2 * H], U8, name="w1_dealt", align_bytes=64)
-        nc.vector.tensor_copy(
-            w1_dealt[:].bitcast(U16).rearrange("p (c t o i) -> p c o t i", c=4, t=4, i=8),
-            w1_raw[:].bitcast(U16).rearrange("p (c o i t) -> p c o t i", c=4, t=4, i=8),
-        )
-
         w_all = keep.tile([P, 4 * 4 * N], F32, name="w_all", tag="late", align_bytes=64)
         w_raw = {}
         for c, w in enumerate((wa, wb)):
             for b in range(2):
                 w_raw[c, b] = w_all[:, (2 * c + b) * 4 * N : (2 * c + b + 1) * 4 * N]
-                nc.sync.dma_start(w_raw[c, b], w[512 * b : 512 * b + 512, :].rearrange("(p j) n -> p (j n)", j=4))
+                w_rows = w[512 * b : 512 * b + 512, :]
+                if (c, b) == (0, 0):
+                    for half in range(2):
+                        nc.sync.dma_start(
+                            w_raw[c, b][:, half * 2 * N : (half + 1) * 2 * N].rearrange("p (j n) -> p j n", j=4),
+                            w_rows[:, half * 256 : (half + 1) * 256].rearrange("(p j) n -> p j n", j=4),
+                        )
+                else:
+                    nc.sync.dma_start(w_raw[c, b], w_rows.rearrange("(p j) n -> p (j n)", j=4))
+
+        w1_dealt = [keep.tile([P, 2 * H], U8, name=f"w1_dealt{b}", align_bytes=64) for b in range(2)]
+
+        def deal_w1(b):
+            nc.vector.tensor_copy(
+                w1_dealt[b][:].bitcast(U16).rearrange("p (a t o i) -> p a o t i", a=2, t=4, i=8),
+                w1_raw[:].bitcast(U16).rearrange("p (a b o i t) -> p b a o t i", a=2, b=2, t=4, i=8)[:, b],
+            )
 
         states = []
         for s in range(2):
-            picked = keep.tile([P, HALF], U32, name=f"picked{s}", align_bytes=64)
+            picked = keep.tile([P, HALF], U32, name="picked", align_bytes=64)
             nc.vector.tensor_copy(picked[:], tab_words[:].bitcast(U32).indirect(offsets[:, 32 * s : 32 * s + 32]))
             parted = keep.tile([P, 2 * 2 * HALF], U8, name=f"parted{s}", align_bytes=64)
             nc.vector.tensor_copy(
@@ -101,6 +114,9 @@ def tile_list_replay_twin_critics_kernel(tc, tab, offs, w1_words, w1_scales, gai
                 picked[:].bitcast(U16).rearrange("p (o i a) -> p o a i", a=2, i=8),
             )
             states.append(parted)
+            if s == 0:
+                deal_w1(0)
+                deal_w1(1)
 
         w_grouped = {}
         w_codes = {}
@@ -116,7 +132,10 @@ def tile_list_replay_twin_critics_kernel(tc, tab, offs, w1_words, w1_scales, gai
         def weave(c, b, half, on_vector):
             cols = slice(half * 64, half * 64 + 64)
             dst = w_grouped[c, b][:].rearrange("p (o i j) -> p o j i", i=4, j=4)[:, cols]
-            src = w_raw[c, b].rearrange("p (j o i) -> p o j i", i=4, j=4)[:, cols]
+            if (c, b) == (0, 0):
+                src = w_raw[c, b][:, half * 2 * N : (half + 1) * 2 * N].rearrange("p (j o i) -> p o j i", i=4, j=4)
+            else:
+                src = w_raw[c, b].rearrange("p (j o i) -> p o j i", i=4, j=4)[:, cols]
             if on_vector:
                 nc.vector.tensor_copy(dst, src)
             else:
@@ -132,15 +151,15 @@ def tile_list_replay_twin_critics_kernel(tc, tab, offs, w1_words, w1_scales, gai
             s, j0 = divmod(q * QUART, HALF)
             tanh_t = ring.tile([P, 2, QUART, 2], F32, name="tanh_t", align_bytes=64)
             for u in range(2):
-                bank = psum.tile([P, 2, QUART], F32, name=f"enc{u}")
+                bank = psum.tile([P, 2, QUART], F32, name="enc", bufs=3)
                 for v in range(2):
                     t = 2 * u + v
                     for a in range(2):
-                        col = a * H + b * 512 + t * P
+                        col = a * 512 + t * P
                         pcol = a * (S + H)
                         nc.tensor.matmul_mx(
                             out=bank[:, v, :],
-                            lhsT=w1_dealt[:, 2 * col : 2 * col + 2 * P].bitcast(FP4X4),
+                            lhsT=w1_dealt[b][:, 2 * col : 2 * col + 2 * P].bitcast(FP4X4),
                             lhsT_scale=planes[:, pcol + S + b * 512 + t * P : pcol + S + b * 512 + (t + 1) * P],
                             rhs=states[s][:, 2 * (a * HALF + j0) : 2 * (a * HALF + j0 + QUART)].bitcast(FP4X4),
                             rhs_scale=planes[:, pcol + q * QUART : pcol + (q + 1) * QUART],
@@ -151,29 +170,37 @@ def tile_list_replay_twin_critics_kernel(tc, tab, offs, w1_words, w1_scales, gai
             tanh_tiles[q, b] = tanh_t
 
         def apply_gain(q, b):
-            grouped = ring.tile([P, QUART * 4], BF16, name="h_grouped", align_bytes=64)
+            grouped = ring.tile([P, QUART, 2, 2], BF16, name="h_grouped", bufs=2, align_bytes=64)
+            split = QUART - GPSIMD_TOKENS[q // 2]
+            values = tanh_tiles[q, b][:].rearrange("p u n v -> p n u v")
             nc.vector.tensor_tensor(
-                grouped[:].rearrange("p (n u v) -> p n u v", u=2, v=2),
-                tanh_tiles[q, b][:].rearrange("p u n v -> p n u v"),
-                gain_t[:, 4 * b : 4 * b + 4].rearrange("p (o u v) -> p o u v", o=1, u=2).to_broadcast([P, QUART, 2, 2]),
+                grouped[:, 0:split],
+                values[:, 0:split],
+                gain_bank[:, :, b : b + 1].rearrange("p (u v) o -> p o u v", u=2).to_broadcast([P, split, 2, 2]),
+                ALU.mult,
+            )
+            nc.gpsimd.tensor_tensor(
+                grouped[:, split:],
+                values[:, split:],
+                gain_t[:, b : b + 1, :].rearrange("p o (u v) -> p o u v", u=2).to_broadcast([P, QUART - split, 2, 2]),
                 ALU.mult,
             )
             h_grouped[q, b] = grouped
 
         def quantise_h(q, b):
             cols = slice(q * QUART, (q + 1) * QUART)
-            nc.vector.quantize_mx(out=h_codes[b][:, cols].bitcast(FP8X4), scales=h_planes[b][:, cols], in_=h_grouped[q, b][:])
+            nc.vector.quantize_mx(out=h_codes[b][:, cols].bitcast(FP8X4), scales=h_planes[b][:, cols], in_=h_grouped[q, b][:].rearrange("p n u v -> p (n u v)"))
 
         def critic_bank(c, j0, width, m0):
             per_bank = 512 // width
             bank = psum.tile([P, per_bank, width], F32, name=f"critic{c}")
             for i in range(per_bank):
-                rows = slice((m0 + i) * P, (m0 + i + 1) * P)
+                cols = slice((m0 + i) * P, (m0 + i + 1) * P)
                 for b in range(2):
                     nc.tensor.matmul_mx(
                         out=bank[:, i, :],
-                        lhsT=w_codes[c, b][:, rows].bitcast(FP8X4),
-                        lhsT_scale=w_planes[c, b][:, rows],
+                        lhsT=w_codes[c, b][:, cols].bitcast(FP8X4),
+                        lhsT_scale=w_planes[c, b][:, cols],
                         rhs=h_codes[b][:, j0 : j0 + width].bitcast(FP8X4),
                         rhs_scale=h_planes[b][:, j0 : j0 + width],
                         start=(b == 0),
@@ -202,49 +229,49 @@ def tile_list_replay_twin_critics_kernel(tc, tab, offs, w1_words, w1_scales, gai
             dst = out.rearrange("(m p) j -> p m j", p=P)[:, m0 : m0 + per_bank, j0 : j0 + width]
             nc.sync.dma_start(dst, res[:])
 
-        encode(0, 0)
-        weave(0, 0, 0, True)
-        weave(0, 0, 1, True)
-        encode(0, 1)
-        apply_gain(0, 0)
+        weave(0, 0, 0, False)
+        weave(0, 0, 1, False)
         quantise_w(0, 0)
-        weave(0, 1, 0, False)
+        encode(0, 0)
+        encode(0, 1)
+        weave(0, 1, 0, True)
+        weave(0, 1, 1, True)
+        quantise_w(0, 1)
+        encode(1, 0)
+        apply_gain(0, 0)
+        encode(1, 1)
         apply_gain(0, 1)
         quantise_h(0, 0)
-        weave(0, 1, 1, False)
-        encode(1, 0)
-        quantise_h(0, 1)
-        quantise_w(0, 1)
         weave(1, 0, 0, False)
-        apply_gain(1, 0)
-        encode(1, 1)
-        weave(1, 0, 1, False)
-        weave(1, 1, 0, True)
-        quantise_h(1, 0)
-        apply_gain(1, 1)
+        weave(1, 0, 1, True)
         quantise_w(1, 0)
-        weave(1, 1, 1, False)
-        quantise_h(1, 1)
         encode(2, 0)
+        apply_gain(1, 0)
+        quantise_h(0, 1)
+        weave(1, 1, 0, False)
+        weave(1, 1, 1, True)
         quantise_w(1, 1)
-        critic_a(0, 512, 0)
-        critic_b(0, 512, 0)
-        apply_gain(2, 0)
         encode(2, 1)
-        critic_a(0, 512, 1)
-        critic_b(0, 512, 1)
-        quantise_h(2, 0)
-        apply_gain(2, 1)
+        apply_gain(1, 1)
+        quantise_h(1, 0)
+        critic_a(0, 256, 0)
+        critic_b(0, 256, 0)
         encode(3, 0)
-        critic_a(0, 512, 2)
-        critic_b(0, 512, 2)
-        quantise_h(2, 1)
-        apply_gain(3, 0)
+        apply_gain(2, 0)
+        quantise_h(1, 1)
+        critic_a(0, 256, 2)
+        critic_b(0, 256, 2)
         encode(3, 1)
-        critic_a(0, 512, 3)
-        critic_b(0, 512, 3)
-        quantise_h(3, 0)
+        apply_gain(2, 1)
+        quantise_h(2, 0)
+        critic_a(256, 256, 0)
+        critic_b(256, 256, 0)
+        apply_gain(3, 0)
+        quantise_h(2, 1)
+        critic_a(256, 256, 2)
+        critic_b(256, 256, 2)
         apply_gain(3, 1)
+        quantise_h(3, 0)
         critic_a(512, 256, 0)
         critic_b(512, 256, 0)
         quantise_h(3, 1)

@@ -18,9 +18,13 @@ ACT = mybir.ActivationFunctionType
 ALU = mybir.AluOpType
 
 P = 128
-HALF = 512
-QUART = 256
-GPSIMD_TOKENS = (80, 112)
+PASS = 512
+HALF = S // 2
+QUART = S // 4
+PIECE = N // 2
+ROW0 = 96
+GPSIMD_TOKENS = (64, 96)
+ENCODER_BANKS = 3
 
 
 def tile_list_replay_twin_critics_kernel(tc, tab, offs, w1_words, w1_scales, gain, wa, ba, wb, bb, out):
@@ -34,93 +38,86 @@ def tile_list_replay_twin_critics_kernel(tc, tab, offs, w1_words, w1_scales, gai
         nc.sync.dma_start(offsets[:], offs)
 
         tab_scales = keep.tile([P, T], U8, name="tab_scales", align_bytes=64)
-        w1s_raw = keep.tile([P, H], U8, name="w1s_raw", align_bytes=64)
+        w1_scale_rows = keep.tile([P, H], U8, name="w1_scale_rows", align_bytes=64)
         nc.sync.dma_start(
-            tab_scales[96:P, :].bitcast(I32),
-            tab[0:1, 512 * T :].rearrange("o (a g t) -> (o g) a t", a=2, g=16).bitcast(I32),
+            tab_scales[ROW0:P, :].bitcast(I32),
+            tab[0:1, PASS * T :].rearrange("o (a g t) -> (o g) a t", a=2, g=16).bitcast(I32),
         )
-        nc.sync.dma_start(w1s_raw[96:P, :].bitcast(I32), w1_scales.rearrange("a g c -> g a c").bitcast(I32))
+        nc.sync.dma_start(w1_scale_rows[ROW0:P, :].bitcast(I32), w1_scales.rearrange("a g c -> g a c").bitcast(I32))
         tab_words = keep.tile([P, T], I32, name="tab_words", align_bytes=64)
-        nc.sync.dma_start(tab_words[:], tab[0:1, 0 : 512 * T].rearrange("o (p x) -> (o p) x", p=P).bitcast(I32))
-        w1_raw = keep.tile([P, 2 * H // 2], I32, name="w1_raw", align_bytes=64)
+        nc.sync.dma_start(tab_words[:], tab[0:1, 0 : PASS * T].rearrange("o (p x) -> (o p) x", p=P).bitcast(I32))
+        w1_raw = keep.tile([P, H], I32, name="w1_raw", align_bytes=64)
         nc.sync.dma_start(w1_raw[:].rearrange("p (a x) -> p a x", a=2), w1_words.rearrange("a p x -> p a x").bitcast(I32))
+        wa_first = keep.tile([P, 4, PIECE], F32, name="wa_first", align_bytes=64)
+        nc.sync.dma_start(wa_first[:], wa[0:PASS, 0:PIECE].rearrange("(p j) n -> p j n", j=4))
 
-        nc.vector.memset(w1s_raw[0:96, :].bitcast(I32), 0)
-        nc.vector.memset(tab_scales[0:96, :].bitcast(I32), 0)
-        rows = keep.tile([P, 512 + P], F32, name="rows")
-        nc.vector.memset(rows[:], 0.0)
+        nc.vector.memset(w1_scale_rows[0:ROW0, :].bitcast(I32), 0)
+        nc.vector.memset(tab_scales[0:ROW0, :].bitcast(I32), 0)
+
+        vectors = keep.tile([P, PASS + P], F32, name="vectors")
+        nc.vector.memset(vectors[:], 0.0)
         planes = keep.tile([P, 2 * (S + H)], U8, name="planes", align_bytes=64)
         nc.vector.memset(planes[:].bitcast(I32), 0)
-        nc.scalar.dma_start(rows[0:2, 0:512], gain.rearrange("(b x) -> b x", b=2))
-        nc.gpsimd.dma_start(rows[0:4, 512:], ba.rearrange("(m p) -> m p", p=P))
-        nc.gpsimd.dma_start(rows[4:8, 512:], bb.rearrange("(m p) -> m p", p=P))
+        nc.scalar.dma_start(vectors[0:2, 0:PASS], gain.rearrange("(b x) -> b x", b=2))
+        nc.gpsimd.dma_start(vectors[0:4, PASS:], ba.rearrange("(m p) -> m p", p=P))
+        nc.gpsimd.dma_start(vectors[4:8, PASS:], bb.rearrange("(m p) -> m p", p=P))
         ident = keep.tile([P, P], F32, name="ident")
         make_identity(nc, ident[:])
-        warm_out = keep.tile([P, 8], F32, name="warm_out")
-        nc.scalar.activation(warm_out[:], ident[:, 0:8], ACT.Tanh)
         gain_bank = psum.tile([P, 4, P], F32, name="gain_bank", bufs=1)
         for t in range(4):
-            nc.tensor.transpose(gain_bank[:, t, :], rows[:, t:512:4], ident[:])
-        gain_t = keep.tile([P, 2, 4], F32, name="gain_t")
-        nc.scalar.copy(gain_t[:], gain_bank[:, :, 0:2].rearrange("p t b -> p b t"))
+            nc.tensor.transpose(gain_bank[:, t, :], vectors[:, t:PASS:4], ident[:])
+        gain_sbuf = keep.tile([P, 2, 4], F32, name="gain_sbuf")
+        nc.scalar.activation(gain_sbuf[:], gain_bank[:, :, 0:2].rearrange("p t b -> p b t"), ACT.Copy)
         bias_bank = psum.tile([P, P], F32, name="critic0")
-        nc.tensor.transpose(bias_bank[:], rows[:, 512:], ident[:])
+        nc.tensor.transpose(bias_bank[:], vectors[:, PASS:], ident[:])
         biases = keep.tile([P, 8], F32, name="biases")
-        nc.scalar.copy(biases[:], bias_bank[:, 0:8])
+        nc.scalar.activation(biases[:], bias_bank[:, 0:8], ACT.Copy)
 
-        spread = keep.tile([P, S + H], U8, name="spread", align_bytes=64)
+        scale_rows = keep.tile([P, S + H], U8, name="scale_rows", align_bytes=64)
         nc.vector.tensor_copy(
-            spread[:, S:].rearrange("p (b t o i) -> p b o t i", b=2, t=4, i=16),
-            w1s_raw[:].rearrange("p (b o i t) -> p b o t i", b=2, t=4, i=16),
+            scale_rows[:, S:].rearrange("p (b t o i) -> p b o t i", b=2, t=4, i=16),
+            w1_scale_rows[:].rearrange("p (b o i t) -> p b o t i", b=2, t=4, i=16),
         )
-        picked_scales = keep.tile([P, S], U8, name="picked_scales", tag="late", align_bytes=64)
+        picked_scales = keep.tile([P, S], U8, name="picked_scales", tag="shared", align_bytes=64)
         nc.vector.tensor_copy(picked_scales[:], tab_scales[:].indirect(offsets[:]))
-        nc.vector.tensor_copy(spread[:, 0:S].bitcast(I32), picked_scales[:].bitcast(I32))
-        for g in range(4):
+        nc.vector.tensor_copy(scale_rows[:, 0:S].bitcast(I32), picked_scales[:].bitcast(I32))
+        for z in range(4):
             nc.sync.dma_start(
-                planes[32 * g : 32 * g + 4, :].bitcast(I32).rearrange("p (a x) -> p a x", a=2),
-                spread[96 + 8 * g : 96 + 8 * g + 8, :].bitcast(I32),
+                planes[32 * z : 32 * z + 4, :].bitcast(I32).rearrange("p (a x) -> p a x", a=2),
+                scale_rows[ROW0 + 8 * z : ROW0 + 8 * z + 8, :].bitcast(I32),
             )
-        w_all = keep.tile([P, 4 * 4 * N], F32, name="w_all", tag="late", align_bytes=64)
-        w_raw = {}
-        for c, w in enumerate((wa, wb)):
-            for b in range(2):
-                w_raw[c, b] = w_all[:, (2 * c + b) * 4 * N : (2 * c + b + 1) * 4 * N]
-                w_rows = w[512 * b : 512 * b + 512, :]
-                if (c, b) == (0, 0):
-                    for half in range(2):
-                        nc.sync.dma_start(
-                            w_raw[c, b][:, half * 2 * N : (half + 1) * 2 * N].rearrange("p (j n) -> p j n", j=4),
-                            w_rows[:, half * 256 : (half + 1) * 256].rearrange("(p j) n -> p j n", j=4),
-                        )
-                else:
-                    nc.sync.dma_start(w_raw[c, b], w_rows.rearrange("(p j) n -> p (j n)", j=4))
+
+        w_rest = keep.tile([P, 4 * PIECE + 3 * 4 * N], F32, name="w_rest", tag="shared", align_bytes=64)
+        wa_second = w_rest[:, 0 : 4 * PIECE].rearrange("p (j n) -> p j n", j=4)
+        nc.sync.dma_start(wa_second, wa[0:PASS, PIECE:N].rearrange("(p j) n -> p j n", j=4))
+        w_pieces = {(0, 0, 0): wa_first[:], (0, 0, 1): wa_second}
+        later_weights = ((0, 1), (1, 0), (1, 1))
+        for i, (c, b) in enumerate(later_weights):
+            loaded = w_rest[:, 4 * PIECE + 4 * N * i : 4 * PIECE + 4 * N * (i + 1)]
+            nc.sync.dma_start(loaded, (wa, wb)[c][PASS * b : PASS * (b + 1), :].rearrange("(p j) n -> p (j n)", j=4))
+            for piece in range(2):
+                w_pieces[c, b, piece] = loaded.rearrange("p (j n) -> p j n", j=4)[:, :, PIECE * piece : PIECE * (piece + 1)]
 
         w1_dealt = [keep.tile([P, 2 * H], U8, name=f"w1_dealt{b}", align_bytes=64) for b in range(2)]
-
-        def deal_w1(b):
-            nc.vector.tensor_copy(
-                w1_dealt[b][:].bitcast(U16).rearrange("p (a t o i) -> p a o t i", a=2, t=4, i=8),
-                w1_raw[:].bitcast(U16).rearrange("p (a b o i t) -> p b a o t i", a=2, b=2, t=4, i=8)[:, b],
-            )
-
         states = []
         for s in range(2):
-            picked = keep.tile([P, HALF], U32, name="picked", align_bytes=64)
-            nc.vector.tensor_copy(picked[:], tab_words[:].bitcast(U32).indirect(offsets[:, 32 * s : 32 * s + 32]))
+            picked_words = keep.tile([P, HALF], U32, name="picked_words", align_bytes=64)
+            list_columns = slice(s * HALF // 16, (s + 1) * HALF // 16)
+            nc.vector.tensor_copy(picked_words[:], tab_words[:].bitcast(U32).indirect(offsets[:, list_columns]))
             parted = keep.tile([P, 2 * 2 * HALF], U8, name=f"parted{s}", align_bytes=64)
             nc.vector.tensor_copy(
                 parted[:].bitcast(U16).rearrange("p (a o i) -> p o a i", a=2, i=8),
-                picked[:].bitcast(U16).rearrange("p (o i a) -> p o a i", a=2, i=8),
+                picked_words[:].bitcast(U16).rearrange("p (o i a) -> p o a i", a=2, i=8),
             )
             states.append(parted)
             if s == 0:
-                deal_w1(0)
-                deal_w1(1)
+                for b in range(2):
+                    nc.vector.tensor_copy(
+                        w1_dealt[b][:].bitcast(U16).rearrange("p (a t o i) -> p a o t i", a=2, t=4, i=8),
+                        w1_raw[:].bitcast(U16).rearrange("p (a b o i t) -> p b a o t i", a=2, b=2, t=4, i=8)[:, b],
+                    )
 
-        w_grouped = {}
-        w_codes = {}
-        w_planes = {}
+        w_grouped, w_codes, w_planes = {}, {}, {}
         for c in range(2):
             for b in range(2):
                 w_grouped[c, b] = keep.tile([P, 4 * N], BF16, name=f"w_grouped{c}{b}", align_bytes=64)
@@ -129,45 +126,41 @@ def tile_list_replay_twin_critics_kernel(tc, tab, offs, w1_words, w1_scales, gai
         h_codes = [keep.tile([P, S], U32, name=f"h_codes{b}", align_bytes=64) for b in range(2)]
         h_planes = [keep.tile([P, S], U8, name=f"h_planes{b}", align_bytes=64) for b in range(2)]
 
-        def weave(c, b, half, on_vector):
-            cols = slice(half * 64, half * 64 + 64)
-            dst = w_grouped[c, b][:].rearrange("p (o i j) -> p o j i", i=4, j=4)[:, cols]
-            if (c, b) == (0, 0):
-                src = w_raw[c, b][:, half * 2 * N : (half + 1) * 2 * N].rearrange("p (j o i) -> p o j i", i=4, j=4)
-            else:
-                src = w_raw[c, b].rearrange("p (j o i) -> p o j i", i=4, j=4)[:, cols]
-            if on_vector:
-                nc.vector.tensor_copy(dst, src)
-            else:
+        def interleave_w(c, b, piece):
+            dst = w_grouped[c, b][:, 4 * PIECE * piece : 4 * PIECE * (piece + 1)].rearrange("p (o i j) -> p o j i", i=4, j=4)
+            src = w_pieces[c, b, piece].rearrange("p j (o i) -> p o j i", i=4)
+            if piece == 0:
                 nc.scalar.copy(dst, src)
+            else:
+                nc.vector.tensor_copy(dst, src)
 
         def quantise_w(c, b):
             nc.vector.quantize_mx(out=w_codes[c, b][:].bitcast(FP8X4), scales=w_planes[c, b][:], in_=w_grouped[c, b][:])
 
-        tanh_tiles = {}
-        h_grouped = {}
+        tanh_tiles, h_grouped = {}, {}
 
         def encode(q, b):
             s, j0 = divmod(q * QUART, HALF)
-            tanh_t = ring.tile([P, 2, QUART, 2], F32, name="tanh_t", align_bytes=64)
+            tanh_tile = ring.tile([P, 2, QUART, 2], F32, name="tanh_tile", align_bytes=64)
             for u in range(2):
-                bank = psum.tile([P, 2, QUART], F32, name="enc", bufs=3)
+                bank = psum.tile([P, 2, QUART], F32, name="encoder", bufs=ENCODER_BANKS)
                 for v in range(2):
                     t = 2 * u + v
                     for a in range(2):
-                        col = a * 512 + t * P
-                        pcol = a * (S + H)
+                        w1_col = a * PASS + t * P
+                        state_col = a * HALF + j0
+                        plane = planes[:, a * (S + H) : (a + 1) * (S + H)]
                         nc.tensor.matmul_mx(
                             out=bank[:, v, :],
-                            lhsT=w1_dealt[b][:, 2 * col : 2 * col + 2 * P].bitcast(FP4X4),
-                            lhsT_scale=planes[:, pcol + S + b * 512 + t * P : pcol + S + b * 512 + (t + 1) * P],
-                            rhs=states[s][:, 2 * (a * HALF + j0) : 2 * (a * HALF + j0 + QUART)].bitcast(FP4X4),
-                            rhs_scale=planes[:, pcol + q * QUART : pcol + (q + 1) * QUART],
+                            lhsT=w1_dealt[b][:, 2 * w1_col : 2 * (w1_col + P)].bitcast(FP4X4),
+                            lhsT_scale=plane[:, S + b * PASS + t * P : S + b * PASS + (t + 1) * P],
+                            rhs=states[s][:, 2 * state_col : 2 * (state_col + QUART)].bitcast(FP4X4),
+                            rhs_scale=plane[:, q * QUART : (q + 1) * QUART],
                             start=(a == 0),
                             stop=(a == 1),
                         )
-                nc.scalar.activation(tanh_t[:, u], bank[:].rearrange("p v n -> p n v"), ACT.Tanh)
-            tanh_tiles[q, b] = tanh_t
+                nc.scalar.activation(tanh_tile[:, u], bank[:].rearrange("p v n -> p n v"), ACT.Tanh)
+            tanh_tiles[q, b] = tanh_tile
 
         def apply_gain(q, b):
             grouped = ring.tile([P, QUART, 2, 2], BF16, name="h_grouped", bufs=2, align_bytes=64)
@@ -182,102 +175,78 @@ def tile_list_replay_twin_critics_kernel(tc, tab, offs, w1_words, w1_scales, gai
             nc.gpsimd.tensor_tensor(
                 grouped[:, split:],
                 values[:, split:],
-                gain_t[:, b : b + 1, :].rearrange("p o (u v) -> p o u v", u=2).to_broadcast([P, QUART - split, 2, 2]),
+                gain_sbuf[:, b : b + 1, :].rearrange("p o (u v) -> p o u v", u=2).to_broadcast([P, QUART - split, 2, 2]),
                 ALU.mult,
             )
             h_grouped[q, b] = grouped
 
         def quantise_h(q, b):
-            cols = slice(q * QUART, (q + 1) * QUART)
-            nc.vector.quantize_mx(out=h_codes[b][:, cols].bitcast(FP8X4), scales=h_planes[b][:, cols], in_=h_grouped[q, b][:].rearrange("p n u v -> p (n u v)"))
+            tokens = slice(q * QUART, (q + 1) * QUART)
+            nc.vector.quantize_mx(
+                out=h_codes[b][:, tokens].bitcast(FP8X4),
+                scales=h_planes[b][:, tokens],
+                in_=h_grouped[q, b][:].rearrange("p n u v -> p (n u v)"),
+            )
 
-        def critic_bank(c, j0, width, m0):
-            per_bank = 512 // width
-            bank = psum.tile([P, per_bank, width], F32, name=f"critic{c}")
-            for i in range(per_bank):
-                cols = slice((m0 + i) * P, (m0 + i + 1) * P)
+        def critic_sums(bank, c, q, m0):
+            tokens = slice(q * QUART, (q + 1) * QUART)
+            for i in range(2):
+                actions = slice((m0 + i) * P, (m0 + i + 1) * P)
                 for b in range(2):
                     nc.tensor.matmul_mx(
                         out=bank[:, i, :],
-                        lhsT=w_codes[c, b][:, cols].bitcast(FP8X4),
-                        lhsT_scale=w_planes[c, b][:, cols],
-                        rhs=h_codes[b][:, j0 : j0 + width].bitcast(FP8X4),
-                        rhs_scale=h_planes[b][:, j0 : j0 + width],
+                        lhsT=w_codes[c, b][:, actions].bitcast(FP8X4),
+                        lhsT_scale=w_planes[c, b][:, actions],
+                        rhs=h_codes[b][:, tokens].bitcast(FP8X4),
+                        rhs_scale=h_planes[b][:, tokens],
                         start=(b == 0),
                         stop=(b == 1),
                     )
-            return bank
 
-        qa_tiles = {}
+        def critics(q, m0):
+            tokens = slice(q * QUART, (q + 1) * QUART)
+            last = q == 3
+            bank_a = psum.tile([P, 2, QUART], F32, name="critic0")
+            critic_sums(bank_a, 0, q, m0)
+            qa = keep.tile([P, 2, QUART], F32, name=f"qa{q}{m0}")
+            for i in range(2):
+                nc.scalar.activation(qa[:, i, :], bank_a[:, i, :], ACT.Identity, bias=biases[:, m0 + i : m0 + i + 1])
+            if last:
+                bank_b = psum.tile([P, 2, QUART], F32, name="encoder", bufs=ENCODER_BANKS)
+            else:
+                bank_b = psum.tile([P, 2, QUART], F32, name="critic1")
+            critic_sums(bank_b, 1, q, m0)
+            result = keep.tile([P, 2, QUART], F32, name=f"result{q}{m0}")
+            for i in range(2):
+                bias_b = biases[:, 4 + m0 + i : 4 + m0 + i + 1]
+                nc.vector.scalar_tensor_tensor(result[:, i, :], bank_b[:, i, :], bias_b, qa[:, i, :], ALU.add, ALU.min)
+                if last:
+                    nc.sync.dma_start(out[(m0 + i) * P : (m0 + i + 1) * P, tokens], result[:, i, :])
+            if not last:
+                nc.sync.dma_start(out.rearrange("(m p) j -> p m j", p=P)[:, m0 : m0 + 2, tokens], result[:])
 
-        def critic_a(j0, width, m0):
-            bank = critic_bank(0, j0, width, m0)
-            per_bank = 512 // width
-            qa = keep.tile([P, per_bank, width], F32, name=f"qa{j0}_{m0}")
-            for i in range(per_bank):
-                nc.scalar.activation(qa[:, i, :], bank[:, i, :], ACT.Identity, bias=biases[:, m0 + i : m0 + i + 1])
-            qa_tiles[j0, m0] = qa
-
-        def critic_b(j0, width, m0):
-            bank = critic_bank(1, j0, width, m0)
-            per_bank = 512 // width
-            res = keep.tile([P, per_bank, width], F32, name=f"res{j0}_{m0}")
-            for i in range(per_bank):
-                nc.vector.scalar_tensor_tensor(
-                    res[:, i, :], bank[:, i, :], biases[:, 4 + m0 + i : 4 + m0 + i + 1], qa_tiles[j0, m0][:, i, :], ALU.add, ALU.min
-                )
-            dst = out.rearrange("(m p) j -> p m j", p=P)[:, m0 : m0 + per_bank, j0 : j0 + width]
-            nc.sync.dma_start(dst, res[:])
-
-        weave(0, 0, 0, False)
-        weave(0, 0, 1, False)
+        units = [(q, b) for q in range(4) for b in range(2)]
+        interleave_w(0, 0, 0)
+        encode(*units[0])
+        encode(*units[1])
+        interleave_w(0, 0, 1)
         quantise_w(0, 0)
-        encode(0, 0)
-        encode(0, 1)
-        weave(0, 1, 0, True)
-        weave(0, 1, 1, True)
-        quantise_w(0, 1)
-        encode(1, 0)
-        apply_gain(0, 0)
-        encode(1, 1)
-        apply_gain(0, 1)
-        quantise_h(0, 0)
-        weave(1, 0, 0, False)
-        weave(1, 0, 1, True)
-        quantise_w(1, 0)
-        encode(2, 0)
-        apply_gain(1, 0)
-        quantise_h(0, 1)
-        weave(1, 1, 0, False)
-        weave(1, 1, 1, True)
-        quantise_w(1, 1)
-        encode(2, 1)
-        apply_gain(1, 1)
-        quantise_h(1, 0)
-        critic_a(0, 256, 0)
-        critic_b(0, 256, 0)
-        encode(3, 0)
-        apply_gain(2, 0)
-        quantise_h(1, 1)
-        critic_a(0, 256, 2)
-        critic_b(0, 256, 2)
-        encode(3, 1)
-        apply_gain(2, 1)
-        quantise_h(2, 0)
-        critic_a(256, 256, 0)
-        critic_b(256, 256, 0)
-        apply_gain(3, 0)
-        quantise_h(2, 1)
-        critic_a(256, 256, 2)
-        critic_b(256, 256, 2)
-        apply_gain(3, 1)
-        quantise_h(3, 0)
-        critic_a(512, 256, 0)
-        critic_b(512, 256, 0)
-        quantise_h(3, 1)
-        critic_a(512, 256, 2)
-        critic_b(512, 256, 2)
-        critic_a(768, 256, 0)
-        critic_b(768, 256, 0)
-        critic_a(768, 256, 2)
-        critic_b(768, 256, 2)
+        ready = []
+        for i, unit in enumerate(units):
+            apply_gain(*unit)
+            if i > 0:
+                quantise_h(*units[i - 1])
+            if i + 2 < len(units):
+                encode(*units[i + 2])
+            if i < len(later_weights):
+                interleave_w(*later_weights[i], 0)
+                interleave_w(*later_weights[i], 1)
+                quantise_w(*later_weights[i])
+            if i > 0 and units[i - 1][1] == 1:
+                ready.extend((units[i - 1][0], m0) for m0 in (0, 2))
+            if i >= len(later_weights):
+                critics(*ready.pop(0))
+        quantise_h(*units[-1])
+        ready.extend((units[-1][0], m0) for m0 in (0, 2))
+        for q, m0 in ready:
+            critics(q, m0)

@@ -23,8 +23,13 @@ HALF = S // 2
 QUART = S // 4
 PIECE = N // 2
 ROW0 = 96
-GPSIMD_TOKENS = (64, 96)
-ENCODER_BANKS = 3
+GROUPS = ((0, HALF), (2 * QUART, QUART), (3 * QUART, QUART))
+UNITS = ((0, 0), (1, 0), (0, 1), (1, 1), (2, 0), (2, 1), (3, 0), (3, 1))
+GPSIMD_TOKENS = (64, 64, 64, 64, 96, 96, 96, 96)
+HBUFS = 2
+SCALAR_COLUMNS = (256, 256, 256, 256)
+PICKED = 1
+BANKS = 7
 
 
 def tile_list_replay_twin_critics_kernel(tc, tab, offs, w1_words, w1_scales, gain, wa, ba, wb, bb, out):
@@ -32,6 +37,7 @@ def tile_list_replay_twin_critics_kernel(tc, tab, offs, w1_words, w1_scales, gai
     with ExitStack() as ctx:
         keep = ctx.enter_context(tc.tile_pool(name="keep", bufs=1))
         ring = ctx.enter_context(tc.tile_pool(name="ring", bufs=3))
+        reused = ctx.enter_context(tc.tile_pool(name="reused", bufs=1))
         psum = ctx.enter_context(tc.psum_pool(name="psum", bufs=2))
 
         offsets = keep.tile([P, S // 16], U16, name="offsets")
@@ -39,46 +45,46 @@ def tile_list_replay_twin_critics_kernel(tc, tab, offs, w1_words, w1_scales, gai
 
         tab_scales = keep.tile([P, T], U8, name="tab_scales", align_bytes=64)
         w1_scale_rows = keep.tile([P, H], U8, name="w1_scale_rows", align_bytes=64)
+        nc.sync.dma_start(w1_scale_rows[ROW0:P, :].bitcast(I32), w1_scales.rearrange("a g c -> g a c").bitcast(I32))
         nc.sync.dma_start(
             tab_scales[ROW0:P, :].bitcast(I32),
             tab[0:1, PASS * T :].rearrange("o (a g t) -> (o g) a t", a=2, g=16).bitcast(I32),
         )
-        nc.sync.dma_start(w1_scale_rows[ROW0:P, :].bitcast(I32), w1_scales.rearrange("a g c -> g a c").bitcast(I32))
         tab_words = keep.tile([P, T], I32, name="tab_words", align_bytes=64)
         nc.sync.dma_start(tab_words[:], tab[0:1, 0 : PASS * T].rearrange("o (p x) -> (o p) x", p=P).bitcast(I32))
         w1_raw = keep.tile([P, H], I32, name="w1_raw", align_bytes=64)
         nc.sync.dma_start(w1_raw[:].rearrange("p (a x) -> p a x", a=2), w1_words.rearrange("a p x -> p a x").bitcast(I32))
-        wa_first = keep.tile([P, 4, PIECE], F32, name="wa_first", align_bytes=64)
-        nc.sync.dma_start(wa_first[:], wa[0:PASS, 0:PIECE].rearrange("(p j) n -> p j n", j=4))
 
         nc.vector.memset(w1_scale_rows[0:ROW0, :].bitcast(I32), 0)
         nc.vector.memset(tab_scales[0:ROW0, :].bitcast(I32), 0)
 
-        vectors = keep.tile([P, PASS + P], F32, name="vectors")
-        nc.vector.memset(vectors[:], 0.0)
+        gain_rows = keep.tile([P, PASS], F32, name="gain_rows")
+        bias_rows = keep.tile([P, P], F32, name="bias_rows")
+        nc.scalar.dma_start(gain_rows[P - 2 : P, :], gain.rearrange("(b x) -> b x", b=2))
+        nc.scalar.dma_start(bias_rows[P - 8 : P - 4, :], ba.rearrange("(m p) -> m p", p=P))
+        nc.scalar.dma_start(bias_rows[P - 4 : P, :], bb.rearrange("(m p) -> m p", p=P))
+        nc.vector.memset(gain_rows[0 : P - 2, :], 0.0)
+        nc.vector.memset(bias_rows[0 : P - 8, :], 0.0)
         planes = keep.tile([P, 2 * (S + H)], U8, name="planes", align_bytes=64)
-        nc.vector.memset(planes[:].bitcast(I32), 0)
-        nc.scalar.dma_start(vectors[0:2, 0:PASS], gain.rearrange("(b x) -> b x", b=2))
-        nc.gpsimd.dma_start(vectors[0:4, PASS:], ba.rearrange("(m p) -> m p", p=P))
-        nc.gpsimd.dma_start(vectors[4:8, PASS:], bb.rearrange("(m p) -> m p", p=P))
+        nc.gpsimd.memset(planes[:].bitcast(I32), 0)
         ident = keep.tile([P, P], F32, name="ident")
         make_identity(nc, ident[:])
         gain_bank = psum.tile([P, 4, P], F32, name="gain_bank", bufs=1)
         for t in range(4):
-            nc.tensor.transpose(gain_bank[:, t, :], vectors[:, t:PASS:4], ident[:])
+            nc.tensor.transpose(gain_bank[:, t, :], gain_rows[:, t:PASS:4], ident[:])
         gain_sbuf = keep.tile([P, 2, 4], F32, name="gain_sbuf")
-        nc.scalar.activation(gain_sbuf[:], gain_bank[:, :, 0:2].rearrange("p t b -> p b t"), ACT.Copy)
-        bias_bank = psum.tile([P, P], F32, name="critic0")
-        nc.tensor.transpose(bias_bank[:], vectors[:, PASS:], ident[:])
+        nc.scalar.activation(gain_sbuf[:], gain_bank[:, :, P - 2 : P].rearrange("p t b -> p b t"), ACT.Copy)
+        bias_bank = psum.tile([P, P], F32, name=f"bank{BANKS - 1}", bufs=1)
+        nc.tensor.transpose(bias_bank[:], bias_rows[:], ident[:])
         biases = keep.tile([P, 8], F32, name="biases")
-        nc.scalar.activation(biases[:], bias_bank[:, 0:8], ACT.Copy)
+        nc.scalar.activation(biases[:], bias_bank[:, P - 8 : P], ACT.Copy)
 
         scale_rows = keep.tile([P, S + H], U8, name="scale_rows", align_bytes=64)
         nc.vector.tensor_copy(
             scale_rows[:, S:].rearrange("p (b t o i) -> p b o t i", b=2, t=4, i=16),
             w1_scale_rows[:].rearrange("p (b o i t) -> p b o t i", b=2, t=4, i=16),
         )
-        picked_scales = keep.tile([P, S], U8, name="picked_scales", tag="shared", align_bytes=64)
+        picked_scales = reused.tile([P, S], U8, name="picked_scales", offset=16 * PIECE - S // 2)
         nc.vector.tensor_copy(picked_scales[:], tab_scales[:].indirect(offsets[:]))
         nc.vector.tensor_copy(scale_rows[:, 0:S].bitcast(I32), picked_scales[:].bitcast(I32))
         for z in range(4):
@@ -87,7 +93,9 @@ def tile_list_replay_twin_critics_kernel(tc, tab, offs, w1_words, w1_scales, gai
                 scale_rows[ROW0 + 8 * z : ROW0 + 8 * z + 8, :].bitcast(I32),
             )
 
-        w_rest = keep.tile([P, 4 * PIECE + 3 * 4 * N], F32, name="w_rest", tag="shared", align_bytes=64)
+        wa_first = reused.tile([P, 4, PIECE], F32, name="wa_first", offset=0)
+        nc.sync.dma_start(wa_first[:], wa[0:PASS, 0:PIECE].rearrange("(p j) n -> p j n", j=4))
+        w_rest = reused.tile([P, 4 * PIECE + 3 * 4 * N], F32, name="w_rest", offset=16 * PIECE)
         wa_second = w_rest[:, 0 : 4 * PIECE].rearrange("p (j n) -> p j n", j=4)
         nc.sync.dma_start(wa_second, wa[0:PASS, PIECE:N].rearrange("(p j) n -> p j n", j=4))
         w_pieces = {(0, 0, 0): wa_first[:], (0, 0, 1): wa_second}
@@ -95,13 +103,14 @@ def tile_list_replay_twin_critics_kernel(tc, tab, offs, w1_words, w1_scales, gai
         for i, (c, b) in enumerate(later_weights):
             loaded = w_rest[:, 4 * PIECE + 4 * N * i : 4 * PIECE + 4 * N * (i + 1)]
             nc.sync.dma_start(loaded, (wa, wb)[c][PASS * b : PASS * (b + 1), :].rearrange("(p j) n -> p (j n)", j=4))
-            for piece in range(2):
-                w_pieces[c, b, piece] = loaded.rearrange("p (j n) -> p j n", j=4)[:, :, PIECE * piece : PIECE * (piece + 1)]
+            split = SCALAR_COLUMNS[2 * c + b]
+            w_pieces[c, b, 0] = loaded.rearrange("p (j n) -> p j n", j=4)[:, :, 0:split]
+            w_pieces[c, b, 1] = loaded.rearrange("p (j n) -> p j n", j=4)[:, :, split:N]
 
         w1_dealt = [keep.tile([P, 2 * H], U8, name=f"w1_dealt{b}", align_bytes=64) for b in range(2)]
         states = []
         for s in range(2):
-            picked_words = keep.tile([P, HALF], U32, name="picked_words", align_bytes=64)
+            picked_words = keep.tile([P, HALF], U32, name="picked_words", bufs=PICKED, align_bytes=64)
             list_columns = slice(s * HALF // 16, (s + 1) * HALF // 16)
             nc.vector.tensor_copy(picked_words[:], tab_words[:].bitcast(U32).indirect(offsets[:, list_columns]))
             parted = keep.tile([P, 2 * 2 * HALF], U8, name=f"parted{s}", align_bytes=64)
@@ -123,11 +132,13 @@ def tile_list_replay_twin_critics_kernel(tc, tab, offs, w1_words, w1_scales, gai
                 w_grouped[c, b] = keep.tile([P, 4 * N], BF16, name=f"w_grouped{c}{b}", align_bytes=64)
                 w_codes[c, b] = keep.tile([P, N], U32, name=f"w_codes{c}{b}", align_bytes=64)
                 w_planes[c, b] = keep.tile([P, N], U8, name=f"w_planes{c}{b}", align_bytes=64)
-        h_codes = [keep.tile([P, S], U32, name=f"h_codes{b}", align_bytes=64) for b in range(2)]
-        h_planes = [keep.tile([P, S], U8, name=f"h_planes{b}", align_bytes=64) for b in range(2)]
+        h_codes = [keep.tile([P, 2 * QUART], U32, name=f"h_codes{g}", align_bytes=64) for g in range(4)]
+        h_planes = [keep.tile([P, 2 * QUART], U8, name=f"h_planes{g}", align_bytes=64) for g in range(4)]
 
         def interleave_w(c, b, piece):
-            dst = w_grouped[c, b][:, 4 * PIECE * piece : 4 * PIECE * (piece + 1)].rearrange("p (o i j) -> p o j i", i=4, j=4)
+            split = SCALAR_COLUMNS[2 * c + b]
+            columns = slice(split, N) if piece else slice(0, split)
+            dst = w_grouped[c, b][:, 4 * columns.start : 4 * columns.stop].rearrange("p (o i j) -> p o j i", i=4, j=4)
             src = w_pieces[c, b, piece].rearrange("p j (o i) -> p o j i", i=4)
             if piece == 0:
                 nc.scalar.copy(dst, src)
@@ -137,116 +148,155 @@ def tile_list_replay_twin_critics_kernel(tc, tab, offs, w1_words, w1_scales, gai
         def quantise_w(c, b):
             nc.vector.quantize_mx(out=w_codes[c, b][:].bitcast(FP8X4), scales=w_planes[c, b][:], in_=w_grouped[c, b][:])
 
-        tanh_tiles, h_grouped = {}, {}
+        banks_taken = []
 
-        def encode(q, b):
-            s, j0 = divmod(q * QUART, HALF)
-            tanh_tile = ring.tile([P, 2, QUART, 2], F32, name="tanh_tile", align_bytes=64)
-            for u in range(2):
-                bank = psum.tile([P, 2, QUART], F32, name="encoder", bufs=ENCODER_BANKS)
-                for v in range(2):
-                    t = 2 * u + v
-                    for a in range(2):
-                        w1_col = a * PASS + t * P
-                        state_col = a * HALF + j0
-                        plane = planes[:, a * (S + H) : (a + 1) * (S + H)]
-                        nc.tensor.matmul_mx(
-                            out=bank[:, v, :],
-                            lhsT=w1_dealt[b][:, 2 * w1_col : 2 * (w1_col + P)].bitcast(FP4X4),
-                            lhsT_scale=plane[:, S + b * PASS + t * P : S + b * PASS + (t + 1) * P],
-                            rhs=states[s][:, 2 * state_col : 2 * (state_col + QUART)].bitcast(FP4X4),
-                            rhs_scale=plane[:, q * QUART : (q + 1) * QUART],
-                            start=(a == 0),
-                            stop=(a == 1),
-                        )
-                nc.scalar.activation(tanh_tile[:, u], bank[:].rearrange("p v n -> p n v"), ACT.Tanh)
-            tanh_tiles[q, b] = tanh_tile
+        def next_bank():
+            banks_taken.append(psum.tile([P, 2 * QUART], F32, name=f"bank{len(banks_taken) % BANKS}", bufs=1))
+            return banks_taken[-1]
 
-        def apply_gain(q, b):
-            grouped = ring.tile([P, QUART, 2, 2], BF16, name="h_grouped", bufs=2, align_bytes=64)
-            split = QUART - GPSIMD_TOKENS[q // 2]
-            values = tanh_tiles[q, b][:].rearrange("p u n v -> p n u v")
+        tanh_tiles, h_grouped, qa_tiles = {}, {}, {}
+
+        def encode(i):
+            g, b = UNITS[i]
+            first, width = g * QUART, QUART
+            if i == 0:
+                tanh_tile = reused.tile([P, 2, width, 2], F32, name="tanh_first", offset=0)
+            else:
+                tanh_tile = keep.tile([P, 2, width, 2], F32, name=f"tanh{g}{b}", align_bytes=64)
+            for n0 in range(0, width, QUART):
+                s, j0 = divmod(first + n0, HALF)
+                for u in range(2):
+                    bank = next_bank()
+                    for v in range(2):
+                        t = 2 * u + v
+                        for a in range(2):
+                            w1_col = a * PASS + t * P
+                            state_col = a * HALF + j0
+                            plane = planes[:, a * (S + H) : (a + 1) * (S + H)]
+                            nc.tensor.matmul_mx(
+                                out=bank[:, v * QUART : (v + 1) * QUART],
+                                lhsT=w1_dealt[b][:, 2 * w1_col : 2 * (w1_col + P)].bitcast(FP4X4),
+                                lhsT_scale=plane[:, S + b * PASS + t * P : S + b * PASS + (t + 1) * P],
+                                rhs=states[s][:, 2 * state_col : 2 * (state_col + QUART)].bitcast(FP4X4),
+                                rhs_scale=plane[:, first + n0 : first + n0 + QUART],
+                                start=(a == 0),
+                                stop=(a == 1),
+                            )
+                    nc.scalar.activation(tanh_tile[:, u, n0 : n0 + QUART], bank[:].rearrange("p (v n) -> p n v", v=2), ACT.Tanh)
+            tanh_tiles[g, b] = tanh_tile
+
+        def apply_gain(i):
+            g, b = UNITS[i]
+            width = QUART
+            pair, side = divmod(i, 2)
+            if side == 0:
+                h_grouped[pair] = ring.tile([P, 2 * 4 * QUART], BF16, name="h_grouped", bufs=HBUFS, align_bytes=64)
+            grouped = h_grouped[pair][:, 4 * QUART * side : 4 * QUART * (side + 1)].rearrange("p (n u v) -> p n u v", u=2, v=2)
+            split = width - GPSIMD_TOKENS[i]
+            values = tanh_tiles[g, b][:].rearrange("p u n v -> p n u v")
             nc.vector.tensor_tensor(
                 grouped[:, 0:split],
                 values[:, 0:split],
-                gain_bank[:, :, b : b + 1].rearrange("p (u v) o -> p o u v", u=2).to_broadcast([P, split, 2, 2]),
+                gain_bank[:, :, P - 2 + b : P - 1 + b].rearrange("p (u v) o -> p o u v", u=2).to_broadcast([P, split, 2, 2]),
                 ALU.mult,
             )
-            nc.gpsimd.tensor_tensor(
-                grouped[:, split:],
-                values[:, split:],
-                gain_sbuf[:, b : b + 1, :].rearrange("p o (u v) -> p o u v", u=2).to_broadcast([P, QUART - split, 2, 2]),
-                ALU.mult,
-            )
-            h_grouped[q, b] = grouped
+            if split < width:
+                nc.gpsimd.tensor_tensor(
+                    grouped[:, split:],
+                    values[:, split:],
+                    gain_sbuf[:, b : b + 1, :].rearrange("p o (u v) -> p o u v", u=2).to_broadcast([P, width - split, 2, 2]),
+                    ALU.mult,
+                )
 
-        def quantise_h(q, b):
-            tokens = slice(q * QUART, (q + 1) * QUART)
-            nc.vector.quantize_mx(
-                out=h_codes[b][:, tokens].bitcast(FP8X4),
-                scales=h_planes[b][:, tokens],
-                in_=h_grouped[q, b][:].rearrange("p n u v -> p (n u v)"),
-            )
+        def quantise_h(g):
+            nc.vector.quantize_mx(out=h_codes[g][:].bitcast(FP8X4), scales=h_planes[g][:], in_=h_grouped[g][:])
 
-        def critic_sums(bank, c, q, m0):
-            tokens = slice(q * QUART, (q + 1) * QUART)
-            for i in range(2):
+        def h_operand(tiles, g, b):
+            return tiles[b][:] if g == 0 else tiles[g + 1][:, b * QUART : (b + 1) * QUART]
+
+        def critic_sums(c, g, m0):
+            first, width = GROUPS[g]
+            bank = next_bank()[:].rearrange("p (i n) -> p i n", n=width)
+            for i in range(2 * QUART // width):
                 actions = slice((m0 + i) * P, (m0 + i + 1) * P)
-                for b in range(2):
+                for b in (1, 0):
                     nc.tensor.matmul_mx(
                         out=bank[:, i, :],
                         lhsT=w_codes[c, b][:, actions].bitcast(FP8X4),
                         lhsT_scale=w_planes[c, b][:, actions],
-                        rhs=h_codes[b][:, tokens].bitcast(FP8X4),
-                        rhs_scale=h_planes[b][:, tokens],
-                        start=(b == 0),
-                        stop=(b == 1),
+                        rhs=h_operand(h_codes, g, b).bitcast(FP8X4),
+                        rhs_scale=h_operand(h_planes, g, b),
+                        start=(b == 1),
+                        stop=(b == 0),
                     )
+            return bank
 
-        def critics(q, m0):
-            tokens = slice(q * QUART, (q + 1) * QUART)
-            last = q == 3
-            bank_a = psum.tile([P, 2, QUART], F32, name="critic0")
-            critic_sums(bank_a, 0, q, m0)
-            qa = keep.tile([P, 2, QUART], F32, name=f"qa{q}{m0}")
-            for i in range(2):
-                nc.scalar.activation(qa[:, i, :], bank_a[:, i, :], ACT.Identity, bias=biases[:, m0 + i : m0 + i + 1])
-            if last:
-                bank_b = psum.tile([P, 2, QUART], F32, name="encoder", bufs=ENCODER_BANKS)
-            else:
-                bank_b = psum.tile([P, 2, QUART], F32, name="critic1")
-            critic_sums(bank_b, 1, q, m0)
-            result = keep.tile([P, 2, QUART], F32, name=f"result{q}{m0}")
-            for i in range(2):
+        def critic_a(g, m0, bank=None):
+            bank = critic_sums(0, g, m0) if bank is None else bank
+            qa = keep.tile(list(bank.shape), F32, name=f"qa{g}{m0}")
+            for i in range(bank.shape[1]):
+                nc.scalar.activation(qa[:, i, :], bank[:, i, :], ACT.Identity, bias=biases[:, m0 + i : m0 + i + 1])
+            qa_tiles[g, m0] = qa
+
+        def critic_b(g, m0, bank=None):
+            first, width = GROUPS[g]
+            bank = critic_sums(1, g, m0) if bank is None else bank
+            tiles = bank.shape[1]
+            result = keep.tile(list(bank.shape), F32, name=f"result{g}{m0}")
+            last = g == len(GROUPS) - 1 and m0 + tiles == 4
+            for i in range(tiles):
                 bias_b = biases[:, 4 + m0 + i : 4 + m0 + i + 1]
-                nc.vector.scalar_tensor_tensor(result[:, i, :], bank_b[:, i, :], bias_b, qa[:, i, :], ALU.add, ALU.min)
+                nc.vector.scalar_tensor_tensor(result[:, i, :], bank[:, i, :], bias_b, qa_tiles[g, m0][:, i, :], ALU.add, ALU.min)
                 if last:
-                    nc.sync.dma_start(out[(m0 + i) * P : (m0 + i + 1) * P, tokens], result[:, i, :])
+                    nc.sync.dma_start(out[(m0 + i) * P : (m0 + i + 1) * P, first : first + width], result[:, i, :])
             if not last:
-                nc.sync.dma_start(out.rearrange("(m p) j -> p m j", p=P)[:, m0 : m0 + 2, tokens], result[:])
+                nc.sync.dma_start(out.rearrange("(m p) j -> p m j", p=P)[:, m0 : m0 + tiles, first : first + width], result[:])
 
-        units = [(q, b) for q in range(4) for b in range(2)]
         interleave_w(0, 0, 0)
-        encode(*units[0])
-        encode(*units[1])
         interleave_w(0, 0, 1)
         quantise_w(0, 0)
-        ready = []
-        for i, unit in enumerate(units):
-            apply_gain(*unit)
-            if i > 0:
-                quantise_h(*units[i - 1])
-            if i + 2 < len(units):
-                encode(*units[i + 2])
-            if i < len(later_weights):
-                interleave_w(*later_weights[i], 0)
-                interleave_w(*later_weights[i], 1)
-                quantise_w(*later_weights[i])
-            if i > 0 and units[i - 1][1] == 1:
-                ready.extend((units[i - 1][0], m0) for m0 in (0, 2))
-            if i >= len(later_weights):
-                critics(*ready.pop(0))
-        quantise_h(*units[-1])
-        ready.extend((units[-1][0], m0) for m0 in (0, 2))
-        for q, m0 in ready:
-            critics(q, m0)
+        interleave_w(0, 1, 0)
+        interleave_w(0, 1, 1)
+        quantise_w(0, 1)
+        encode(0)
+        encode(1)
+        apply_gain(0)
+        encode(2)
+        apply_gain(1)
+        encode(3)
+        apply_gain(2)
+        quantise_h(0)
+        interleave_w(1, 0, 0)
+        interleave_w(1, 0, 1)
+        quantise_w(1, 0)
+        encode(4)
+        interleave_w(1, 1, 0)
+        interleave_w(1, 1, 1)
+        apply_gain(3)
+        quantise_w(1, 1)
+        encode(5)
+        quantise_h(1)
+        encode(6)
+        encode(7)
+        critic_a(0, 0)
+        critic_a(0, 1)
+        apply_gain(4)
+        critic_b(0, 0)
+        critic_a(0, 2)
+        critic_b(0, 1)
+        apply_gain(5)
+        critic_a(0, 3)
+        critic_b(0, 2)
+        apply_gain(6)
+        quantise_h(2)
+        critic_b(0, 3)
+        apply_gain(7)
+        critic_a(1, 0)
+        quantise_h(3)
+        critic_b(1, 0)
+        critic_a(1, 2)
+        critic_b(1, 2)
+        critic_a(2, 0)
+        critic_b(2, 0)
+        critic_a(2, 2)
+        critic_b(2, 2)

@@ -27,6 +27,7 @@ GROUPS = ((0, HALF), (2 * QUART, QUART), (3 * QUART, QUART))
 UNITS = ((0, 0), (1, 0), (0, 1), (1, 1), (2, 0), (2, 1), (3, 0), (3, 1))
 GPSIMD_TOKENS = (64, 64, 64, 64, 96, 96, 96, 96)
 HBUFS = 2
+EARLY_BYTES = 8 * 16 * QUART
 SCALAR_COLUMNS = (256, 256, 256, 256)
 PICKED = 1
 BANKS = 7
@@ -84,7 +85,7 @@ def tile_list_replay_twin_critics_kernel(tc, tab, offs, w1_words, w1_scales, gai
             scale_rows[:, S:].rearrange("p (b t o i) -> p b o t i", b=2, t=4, i=16),
             w1_scale_rows[:].rearrange("p (b o i t) -> p b o t i", b=2, t=4, i=16),
         )
-        picked_scales = reused.tile([P, S], U8, name="picked_scales", offset=16 * PIECE - S // 2)
+        picked_scales = reused.tile([P, S], U8, name="picked_scales", offset=EARLY_BYTES - S // 2)
         nc.vector.tensor_copy(picked_scales[:], tab_scales[:].indirect(offsets[:]))
         nc.vector.tensor_copy(scale_rows[:, 0:S].bitcast(I32), picked_scales[:].bitcast(I32))
         for z in range(4):
@@ -93,9 +94,9 @@ def tile_list_replay_twin_critics_kernel(tc, tab, offs, w1_words, w1_scales, gai
                 scale_rows[ROW0 + 8 * z : ROW0 + 8 * z + 8, :].bitcast(I32),
             )
 
-        wa_first = reused.tile([P, 4, PIECE], F32, name="wa_first", offset=0)
+        wa_first = reused.tile([P, 4, PIECE], F32, name="wa_first", offset=EARLY_BYTES - 16 * PIECE)
         nc.sync.dma_start(wa_first[:], wa[0:PASS, 0:PIECE].rearrange("(p j) n -> p j n", j=4))
-        w_rest = reused.tile([P, 4 * PIECE + 3 * 4 * N], F32, name="w_rest", offset=16 * PIECE)
+        w_rest = reused.tile([P, 4 * PIECE + 3 * 4 * N], F32, name="w_rest", offset=EARLY_BYTES)
         wa_second = w_rest[:, 0 : 4 * PIECE].rearrange("p (j n) -> p j n", j=4)
         nc.sync.dma_start(wa_second, wa[0:PASS, PIECE:N].rearrange("(p j) n -> p j n", j=4))
         w_pieces = {(0, 0, 0): wa_first[:], (0, 0, 1): wa_second}
@@ -155,14 +156,12 @@ def tile_list_replay_twin_critics_kernel(tc, tab, offs, w1_words, w1_scales, gai
             return banks_taken[-1]
 
         tanh_tiles, h_grouped, qa_tiles = {}, {}, {}
+        tanh_values = reused.tile([P, len(UNITS) * 4 * QUART], F32, name="tanh_values", offset=0)
 
         def encode(i):
             g, b = UNITS[i]
             first, width = g * QUART, QUART
-            if i == 0:
-                tanh_tile = reused.tile([P, 2, width, 2], F32, name="tanh_first", offset=0)
-            else:
-                tanh_tile = keep.tile([P, 2, width, 2], F32, name=f"tanh{g}{b}", align_bytes=64)
+            tanh_tile = tanh_values[:, 4 * QUART * i : 4 * QUART * (i + 1)].rearrange("p (u n v) -> p u n v", u=2, v=2)
             for n0 in range(0, width, QUART):
                 s, j0 = divmod(first + n0, HALF)
                 for u in range(2):
@@ -193,7 +192,7 @@ def tile_list_replay_twin_critics_kernel(tc, tab, offs, w1_words, w1_scales, gai
                 h_grouped[pair] = ring.tile([P, 2 * 4 * QUART], BF16, name="h_grouped", bufs=HBUFS, align_bytes=64)
             grouped = h_grouped[pair][:, 4 * QUART * side : 4 * QUART * (side + 1)].rearrange("p (n u v) -> p n u v", u=2, v=2)
             split = width - GPSIMD_TOKENS[i]
-            values = tanh_tiles[g, b][:].rearrange("p u n v -> p n u v")
+            values = tanh_tiles[g, b].rearrange("p u n v -> p n u v")
             nc.vector.tensor_tensor(
                 grouped[:, 0:split],
                 values[:, 0:split],

@@ -23,23 +23,20 @@ HALF = S // 2
 QUART = S // 4
 PIECE = N // 2
 ROW0 = 96
-GROUPS = ((0, HALF), (2 * QUART, QUART), (3 * QUART, QUART))
-UNITS = ((0, 0), (1, 0), (0, 1), (1, 1), (2, 0), (2, 1), (3, 0), (3, 1))
-GPSIMD_TOKENS = (64, 64, 64, 64, 96, 96, 96, 96)
-HBUFS = 2
-EARLY_BYTES = 8 * 16 * QUART
-SCALAR_COLUMNS = (256, 256, 256, 256)
-PICKED = 1
 BANKS = 7
+UNITS = ((0, 0), (1, 0), (0, 1), (1, 1), (2, 0), (2, 1), (3, 0), (3, 1))
+GROUPS = ((0, HALF), (2 * QUART, QUART), (3 * QUART, QUART))
+GPSIMD_TOKENS = (80, 112)
+TANH_BYTES = len(UNITS) * 4 * QUART * 4
 
 
 def tile_list_replay_twin_critics_kernel(tc, tab, offs, w1_words, w1_scales, gain, wa, ba, wb, bb, out):
     nc = tc.nc
     with ExitStack() as ctx:
         keep = ctx.enter_context(tc.tile_pool(name="keep", bufs=1))
-        ring = ctx.enter_context(tc.tile_pool(name="ring", bufs=3))
+        ring = ctx.enter_context(tc.tile_pool(name="ring", bufs=2))
         reused = ctx.enter_context(tc.tile_pool(name="reused", bufs=1))
-        psum = ctx.enter_context(tc.psum_pool(name="psum", bufs=2))
+        psum = ctx.enter_context(tc.psum_pool(name="psum", bufs=1))
 
         offsets = keep.tile([P, S // 16], U16, name="offsets")
         nc.sync.dma_start(offsets[:], offs)
@@ -70,12 +67,12 @@ def tile_list_replay_twin_critics_kernel(tc, tab, offs, w1_words, w1_scales, gai
         nc.gpsimd.memset(planes[:].bitcast(I32), 0)
         ident = keep.tile([P, P], F32, name="ident")
         make_identity(nc, ident[:])
-        gain_bank = psum.tile([P, 4, P], F32, name="gain_bank", bufs=1)
+        gain_bank = psum.tile([P, 4, P], F32, name="gain_bank")
         for t in range(4):
             nc.tensor.transpose(gain_bank[:, t, :], gain_rows[:, t:PASS:4], ident[:])
         gain_sbuf = keep.tile([P, 2, 4], F32, name="gain_sbuf")
         nc.scalar.activation(gain_sbuf[:], gain_bank[:, :, P - 2 : P].rearrange("p t b -> p b t"), ACT.Copy)
-        bias_bank = psum.tile([P, P], F32, name=f"bank{BANKS - 1}", bufs=1)
+        bias_bank = psum.tile([P, P], F32, name=f"bank{BANKS - 1}")
         nc.tensor.transpose(bias_bank[:], bias_rows[:], ident[:])
         biases = keep.tile([P, 8], F32, name="biases")
         nc.scalar.activation(biases[:], bias_bank[:, P - 8 : P], ACT.Copy)
@@ -85,7 +82,7 @@ def tile_list_replay_twin_critics_kernel(tc, tab, offs, w1_words, w1_scales, gai
             scale_rows[:, S:].rearrange("p (b t o i) -> p b o t i", b=2, t=4, i=16),
             w1_scale_rows[:].rearrange("p (b o i t) -> p b o t i", b=2, t=4, i=16),
         )
-        picked_scales = reused.tile([P, S], U8, name="picked_scales", offset=EARLY_BYTES - S // 2)
+        picked_scales = reused.tile([P, S], U8, name="picked_scales", offset=TANH_BYTES - S // 2)
         nc.vector.tensor_copy(picked_scales[:], tab_scales[:].indirect(offsets[:]))
         nc.vector.tensor_copy(scale_rows[:, 0:S].bitcast(I32), picked_scales[:].bitcast(I32))
         for z in range(4):
@@ -94,38 +91,60 @@ def tile_list_replay_twin_critics_kernel(tc, tab, offs, w1_words, w1_scales, gai
                 scale_rows[ROW0 + 8 * z : ROW0 + 8 * z + 8, :].bitcast(I32),
             )
 
-        wa_first = reused.tile([P, 4, PIECE], F32, name="wa_first", offset=EARLY_BYTES - 16 * PIECE)
+        wa_first = reused.tile([P, 4, PIECE], F32, name="wa_first", offset=TANH_BYTES - 4 * PIECE * 4)
         nc.sync.dma_start(wa_first[:], wa[0:PASS, 0:PIECE].rearrange("(p j) n -> p j n", j=4))
-        w_rest = reused.tile([P, 4 * PIECE + 3 * 4 * N], F32, name="w_rest", offset=EARLY_BYTES)
+        w_rest = reused.tile([P, 4 * PIECE + 3 * 4 * N], F32, name="w_rest", offset=TANH_BYTES)
         wa_second = w_rest[:, 0 : 4 * PIECE].rearrange("p (j n) -> p j n", j=4)
         nc.sync.dma_start(wa_second, wa[0:PASS, PIECE:N].rearrange("(p j) n -> p j n", j=4))
         w_pieces = {(0, 0, 0): wa_first[:], (0, 0, 1): wa_second}
-        later_weights = ((0, 1), (1, 0), (1, 1))
-        for i, (c, b) in enumerate(later_weights):
+        for i, (c, b) in enumerate(((0, 1), (1, 0), (1, 1))):
             loaded = w_rest[:, 4 * PIECE + 4 * N * i : 4 * PIECE + 4 * N * (i + 1)]
             nc.sync.dma_start(loaded, (wa, wb)[c][PASS * b : PASS * (b + 1), :].rearrange("(p j) n -> p (j n)", j=4))
-            split = SCALAR_COLUMNS[2 * c + b]
-            w_pieces[c, b, 0] = loaded.rearrange("p (j n) -> p j n", j=4)[:, :, 0:split]
-            w_pieces[c, b, 1] = loaded.rearrange("p (j n) -> p j n", j=4)[:, :, split:N]
+            for piece in range(2):
+                w_pieces[c, b, piece] = loaded.rearrange("p (j n) -> p j n", j=4)[:, :, PIECE * piece : PIECE * (piece + 1)]
 
         w1_dealt = [keep.tile([P, 2 * H], U8, name=f"w1_dealt{b}", align_bytes=64) for b in range(2)]
+        warm_bank = psum.tile([P, PASS], F32, name=f"bank{BANKS - 2}")
+        w1_bytes = w1_raw[:].bitcast(U8)
+        for i in range(2):
+            nc.tensor.matmul_mx(
+                out=warm_bank[:],
+                lhsT=w1_bytes[:, 0 : 2 * P].bitcast(FP4X4),
+                lhsT_scale=w1_scale_rows[:, 0:P],
+                rhs=w1_bytes[:, 0 : 2 * PASS].bitcast(FP4X4),
+                rhs_scale=w1_scale_rows[:, 0:PASS],
+                start=True,
+                stop=True,
+            )
         states = []
+
+        def part(parted, picked_words, first, count):
+            groups = slice(first // 8, (first + count) // 8)
+            nc.vector.tensor_copy(
+                parted[:].bitcast(U16).rearrange("p (a o i) -> p o a i", a=2, i=8)[:, groups],
+                picked_words[:].bitcast(U16).rearrange("p (o i a) -> p o a i", a=2, i=8)[:, groups],
+            )
+
+        def deal(b, slots):
+            nc.vector.tensor_copy(
+                w1_dealt[b][:].bitcast(U16).rearrange("p (a t o i) -> p a o t i", a=2, t=4, i=8)[:, :, :, slots],
+                w1_raw[:].bitcast(U16).rearrange("p (a b o i t) -> p b a o t i", a=2, b=2, t=4, i=8)[:, b, :, :, slots],
+            )
+
         for s in range(2):
-            picked_words = keep.tile([P, HALF], U32, name="picked_words", bufs=PICKED, align_bytes=64)
+            picked_words = keep.tile([P, HALF], U32, name="picked_words", align_bytes=64)
             list_columns = slice(s * HALF // 16, (s + 1) * HALF // 16)
             nc.vector.tensor_copy(picked_words[:], tab_words[:].bitcast(U32).indirect(offsets[:, list_columns]))
             parted = keep.tile([P, 2 * 2 * HALF], U8, name=f"parted{s}", align_bytes=64)
-            nc.vector.tensor_copy(
-                parted[:].bitcast(U16).rearrange("p (a o i) -> p o a i", a=2, i=8),
-                picked_words[:].bitcast(U16).rearrange("p (o i a) -> p o a i", a=2, i=8),
-            )
-            states.append(parted)
             if s == 0:
-                for b in range(2):
-                    nc.vector.tensor_copy(
-                        w1_dealt[b][:].bitcast(U16).rearrange("p (a t o i) -> p a o t i", a=2, t=4, i=8),
-                        w1_raw[:].bitcast(U16).rearrange("p (a b o i t) -> p b a o t i", a=2, b=2, t=4, i=8)[:, b],
-                    )
+                deal(0, slice(0, 2))
+                part(parted, picked_words, 0, QUART)
+                deal(0, slice(2, 4))
+                part(parted, picked_words, QUART, QUART)
+                deal(1, slice(0, 4))
+            else:
+                part(parted, picked_words, 0, HALF)
+            states.append(parted)
 
         w_grouped, w_codes, w_planes = {}, {}, {}
         for c in range(2):
@@ -133,90 +152,80 @@ def tile_list_replay_twin_critics_kernel(tc, tab, offs, w1_words, w1_scales, gai
                 w_grouped[c, b] = keep.tile([P, 4 * N], BF16, name=f"w_grouped{c}{b}", align_bytes=64)
                 w_codes[c, b] = keep.tile([P, N], U32, name=f"w_codes{c}{b}", align_bytes=64)
                 w_planes[c, b] = keep.tile([P, N], U8, name=f"w_planes{c}{b}", align_bytes=64)
-        h_codes = [keep.tile([P, 2 * QUART], U32, name=f"h_codes{g}", align_bytes=64) for g in range(4)]
-        h_planes = [keep.tile([P, 2 * QUART], U8, name=f"h_planes{g}", align_bytes=64) for g in range(4)]
+        h_codes = [keep.tile([P, 2 * QUART], U32, name=f"h_codes{pair}", align_bytes=64) for pair in range(4)]
+        h_planes = [keep.tile([P, 2 * QUART], U8, name=f"h_planes{pair}", align_bytes=64) for pair in range(4)]
 
-        def interleave_w(c, b, piece):
-            split = SCALAR_COLUMNS[2 * c + b]
-            columns = slice(split, N) if piece else slice(0, split)
-            dst = w_grouped[c, b][:, 4 * columns.start : 4 * columns.stop].rearrange("p (o i j) -> p o j i", i=4, j=4)
-            src = w_pieces[c, b, piece].rearrange("p j (o i) -> p o j i", i=4)
-            if piece == 0:
-                nc.scalar.copy(dst, src)
-            else:
-                nc.vector.tensor_copy(dst, src)
-
-        def quantise_w(c, b):
+        def prepare_w(c, b):
+            for piece, copy in enumerate((nc.scalar.copy, nc.vector.tensor_copy)):
+                copy(
+                    w_grouped[c, b][:, 4 * PIECE * piece : 4 * PIECE * (piece + 1)].rearrange("p (o i j) -> p o j i", i=4, j=4),
+                    w_pieces[c, b, piece].rearrange("p j (o i) -> p o j i", i=4),
+                )
             nc.vector.quantize_mx(out=w_codes[c, b][:].bitcast(FP8X4), scales=w_planes[c, b][:], in_=w_grouped[c, b][:])
 
         banks_taken = []
 
         def next_bank():
-            banks_taken.append(psum.tile([P, 2 * QUART], F32, name=f"bank{len(banks_taken) % BANKS}", bufs=1))
+            banks_taken.append(psum.tile([P, 2 * QUART], F32, name=f"bank{len(banks_taken) % BANKS}"))
             return banks_taken[-1]
 
-        tanh_tiles, h_grouped, qa_tiles = {}, {}, {}
         tanh_values = reused.tile([P, len(UNITS) * 4 * QUART], F32, name="tanh_values", offset=0)
+        h_grouped, qa_tiles = {}, {}
+
+        def tanh_of(i):
+            return tanh_values[:, 4 * QUART * i : 4 * QUART * (i + 1)].rearrange("p (u n v) -> p u n v", u=2, v=2)
 
         def encode(i):
-            g, b = UNITS[i]
-            first, width = g * QUART, QUART
-            tanh_tile = tanh_values[:, 4 * QUART * i : 4 * QUART * (i + 1)].rearrange("p (u n v) -> p u n v", u=2, v=2)
-            for n0 in range(0, width, QUART):
-                s, j0 = divmod(first + n0, HALF)
-                for u in range(2):
-                    bank = next_bank()
-                    for v in range(2):
-                        t = 2 * u + v
-                        for a in range(2):
-                            w1_col = a * PASS + t * P
-                            state_col = a * HALF + j0
-                            plane = planes[:, a * (S + H) : (a + 1) * (S + H)]
-                            nc.tensor.matmul_mx(
-                                out=bank[:, v * QUART : (v + 1) * QUART],
-                                lhsT=w1_dealt[b][:, 2 * w1_col : 2 * (w1_col + P)].bitcast(FP4X4),
-                                lhsT_scale=plane[:, S + b * PASS + t * P : S + b * PASS + (t + 1) * P],
-                                rhs=states[s][:, 2 * state_col : 2 * (state_col + QUART)].bitcast(FP4X4),
-                                rhs_scale=plane[:, first + n0 : first + n0 + QUART],
-                                start=(a == 0),
-                                stop=(a == 1),
-                            )
-                    nc.scalar.activation(tanh_tile[:, u, n0 : n0 + QUART], bank[:].rearrange("p (v n) -> p n v", v=2), ACT.Tanh)
-            tanh_tiles[g, b] = tanh_tile
+            q, b = UNITS[i]
+            s, j0 = divmod(q * QUART, HALF)
+            for u in range(2):
+                bank = next_bank()
+                for v in range(2):
+                    t = 2 * u + v
+                    for a in range(2):
+                        w1_col = a * PASS + t * P
+                        state_col = a * HALF + j0
+                        plane = planes[:, a * (S + H) : (a + 1) * (S + H)]
+                        nc.tensor.matmul_mx(
+                            out=bank[:, v * QUART : (v + 1) * QUART],
+                            lhsT=w1_dealt[b][:, 2 * w1_col : 2 * (w1_col + P)].bitcast(FP4X4),
+                            lhsT_scale=plane[:, S + b * PASS + t * P : S + b * PASS + (t + 1) * P],
+                            rhs=states[s][:, 2 * state_col : 2 * (state_col + QUART)].bitcast(FP4X4),
+                            rhs_scale=plane[:, q * QUART : (q + 1) * QUART],
+                            start=(a == 0),
+                            stop=(a == 1),
+                        )
+                nc.scalar.activation(tanh_of(i)[:, u], bank[:].rearrange("p (v n) -> p n v", v=2), ACT.Tanh)
 
-        def apply_gain(i):
-            g, b = UNITS[i]
-            width = QUART
+        def make_h(i):
+            b = UNITS[i][1]
             pair, side = divmod(i, 2)
             if side == 0:
-                h_grouped[pair] = ring.tile([P, 2 * 4 * QUART], BF16, name="h_grouped", bufs=HBUFS, align_bytes=64)
+                h_grouped[pair] = ring.tile([P, 2 * 4 * QUART], BF16, name="h_grouped", align_bytes=64)
             grouped = h_grouped[pair][:, 4 * QUART * side : 4 * QUART * (side + 1)].rearrange("p (n u v) -> p n u v", u=2, v=2)
-            split = width - GPSIMD_TOKENS[i]
-            values = tanh_tiles[g, b].rearrange("p u n v -> p n u v")
+            split = QUART - GPSIMD_TOKENS[i // 4]
+            values = tanh_of(i).rearrange("p u n v -> p n u v")
             nc.vector.tensor_tensor(
                 grouped[:, 0:split],
                 values[:, 0:split],
                 gain_bank[:, :, P - 2 + b : P - 1 + b].rearrange("p (u v) o -> p o u v", u=2).to_broadcast([P, split, 2, 2]),
                 ALU.mult,
             )
-            if split < width:
-                nc.gpsimd.tensor_tensor(
-                    grouped[:, split:],
-                    values[:, split:],
-                    gain_sbuf[:, b : b + 1, :].rearrange("p o (u v) -> p o u v", u=2).to_broadcast([P, width - split, 2, 2]),
-                    ALU.mult,
-                )
-
-        def quantise_h(g):
-            nc.vector.quantize_mx(out=h_codes[g][:].bitcast(FP8X4), scales=h_planes[g][:], in_=h_grouped[g][:])
+            nc.gpsimd.tensor_tensor(
+                grouped[:, split:],
+                values[:, split:],
+                gain_sbuf[:, b : b + 1, :].rearrange("p o (u v) -> p o u v", u=2).to_broadcast([P, QUART - split, 2, 2]),
+                ALU.mult,
+            )
+            if side == 1:
+                nc.vector.quantize_mx(out=h_codes[pair][:].bitcast(FP8X4), scales=h_planes[pair][:], in_=h_grouped[pair][:])
 
         def h_operand(tiles, g, b):
             return tiles[b][:] if g == 0 else tiles[g + 1][:, b * QUART : (b + 1) * QUART]
 
         def critic_sums(c, g, m0):
-            first, width = GROUPS[g]
-            bank = next_bank()[:].rearrange("p (i n) -> p i n", n=width)
-            for i in range(2 * QUART // width):
+            bank = next_bank()[:].rearrange("p (i n) -> p i n", n=GROUPS[g][1])
+            for i in range(bank.shape[1]):
                 actions = slice((m0 + i) * P, (m0 + i + 1) * P)
                 for b in (1, 0):
                     nc.tensor.matmul_mx(
@@ -230,72 +239,42 @@ def tile_list_replay_twin_critics_kernel(tc, tab, offs, w1_words, w1_scales, gai
                     )
             return bank
 
-        def critic_a(g, m0, bank=None):
-            bank = critic_sums(0, g, m0) if bank is None else bank
-            qa = keep.tile(list(bank.shape), F32, name=f"qa{g}{m0}")
+        def critic_a(g, m0):
+            bank = critic_sums(0, g, m0)
+            qa_tiles[g, m0] = keep.tile(list(bank.shape), F32, name=f"qa{g}{m0}")
             for i in range(bank.shape[1]):
-                nc.scalar.activation(qa[:, i, :], bank[:, i, :], ACT.Identity, bias=biases[:, m0 + i : m0 + i + 1])
-            qa_tiles[g, m0] = qa
+                nc.scalar.activation(qa_tiles[g, m0][:, i, :], bank[:, i, :], ACT.Identity, bias=biases[:, m0 + i : m0 + i + 1])
 
-        def critic_b(g, m0, bank=None):
-            first, width = GROUPS[g]
-            bank = critic_sums(1, g, m0) if bank is None else bank
+        def critic_b(g, m0):
+            bank = critic_sums(1, g, m0)
             tiles = bank.shape[1]
+            tokens = slice(GROUPS[g][0], GROUPS[g][0] + GROUPS[g][1])
             result = keep.tile(list(bank.shape), F32, name=f"result{g}{m0}")
-            last = g == len(GROUPS) - 1 and m0 + tiles == 4
+            last = g == len(GROUPS) - 1 and m0 + tiles == N // P
             for i in range(tiles):
                 bias_b = biases[:, 4 + m0 + i : 4 + m0 + i + 1]
                 nc.vector.scalar_tensor_tensor(result[:, i, :], bank[:, i, :], bias_b, qa_tiles[g, m0][:, i, :], ALU.add, ALU.min)
                 if last:
-                    nc.sync.dma_start(out[(m0 + i) * P : (m0 + i + 1) * P, first : first + width], result[:, i, :])
+                    nc.sync.dma_start(out[(m0 + i) * P : (m0 + i + 1) * P, tokens], result[:, i, :])
             if not last:
-                nc.sync.dma_start(out.rearrange("(m p) j -> p m j", p=P)[:, m0 : m0 + tiles, first : first + width], result[:])
+                nc.sync.dma_start(out.rearrange("(m p) j -> p m j", p=P)[:, m0 : m0 + tiles, tokens], result[:])
 
-        interleave_w(0, 0, 0)
-        interleave_w(0, 0, 1)
-        quantise_w(0, 0)
-        interleave_w(0, 1, 0)
-        interleave_w(0, 1, 1)
-        quantise_w(0, 1)
-        encode(0)
-        encode(1)
-        apply_gain(0)
-        encode(2)
-        apply_gain(1)
-        encode(3)
-        apply_gain(2)
-        quantise_h(0)
-        interleave_w(1, 0, 0)
-        interleave_w(1, 0, 1)
-        quantise_w(1, 0)
-        encode(4)
-        interleave_w(1, 1, 0)
-        interleave_w(1, 1, 1)
-        apply_gain(3)
-        quantise_w(1, 1)
-        encode(5)
-        quantise_h(1)
-        encode(6)
-        encode(7)
-        critic_a(0, 0)
-        critic_a(0, 1)
-        apply_gain(4)
-        critic_b(0, 0)
-        critic_a(0, 2)
-        critic_b(0, 1)
-        apply_gain(5)
-        critic_a(0, 3)
-        critic_b(0, 2)
-        apply_gain(6)
-        quantise_h(2)
-        critic_b(0, 3)
-        apply_gain(7)
-        critic_a(1, 0)
-        quantise_h(3)
-        critic_b(1, 0)
-        critic_a(1, 2)
-        critic_b(1, 2)
-        critic_a(2, 0)
-        critic_b(2, 0)
-        critic_a(2, 2)
-        critic_b(2, 2)
+        for b in range(2):
+            prepare_w(0, b)
+        for i in range(4):
+            encode(i)
+            make_h(i)
+        for b in range(2):
+            prepare_w(1, b)
+            encode(4 + b)
+        for i in range(6, len(UNITS)):
+            encode(i)
+        for m in range(N // P):
+            critic_a(0, m)
+        for m in range(N // P):
+            make_h(4 + m)
+            critic_b(0, m)
+        for g in range(1, len(GROUPS)):
+            for m0 in (0, 2):
+                critic_a(g, m0)
+                critic_b(g, m0)

@@ -22,6 +22,7 @@ PASS = 512
 HALF = S // 2
 QUART = S // 4
 PIECE = N // 2
+SCALAR_COLUMNS = (128, 256, 256)
 ROW0 = 96
 BANKS = 7
 UNITS = ((0, 0), (1, 0), (0, 1), (1, 1), (2, 0), (2, 1), (3, 0), (3, 1))
@@ -43,11 +44,11 @@ def tile_list_replay_twin_critics_kernel(tc, tab, offs, w1_words, w1_scales, gai
 
         tab_scales = keep.tile([P, T], U8, name="tab_scales", align_bytes=64)
         w1_scale_rows = keep.tile([P, H], U8, name="w1_scale_rows", align_bytes=64)
-        nc.sync.dma_start(w1_scale_rows[ROW0:P, :].bitcast(I32), w1_scales.rearrange("a g c -> g a c").bitcast(I32))
         nc.sync.dma_start(
             tab_scales[ROW0:P, :].bitcast(I32),
             tab[0:1, PASS * T :].rearrange("o (a g t) -> (o g) a t", a=2, g=16).bitcast(I32),
         )
+        nc.sync.dma_start(w1_scale_rows[ROW0:P, :].bitcast(I32), w1_scales.rearrange("a g c -> g a c").bitcast(I32))
         tab_words = keep.tile([P, T], I32, name="tab_words", align_bytes=64)
         nc.sync.dma_start(tab_words[:], tab[0:1, 0 : PASS * T].rearrange("o (p x) -> (o p) x", p=P).bitcast(I32))
         w1_raw = keep.tile([P, H], I32, name="w1_raw", align_bytes=64)
@@ -100,22 +101,10 @@ def tile_list_replay_twin_critics_kernel(tc, tab, offs, w1_words, w1_scales, gai
         for i, (c, b) in enumerate(((0, 1), (1, 0), (1, 1))):
             loaded = w_rest[:, 4 * PIECE + 4 * N * i : 4 * PIECE + 4 * N * (i + 1)]
             nc.sync.dma_start(loaded, (wa, wb)[c][PASS * b : PASS * (b + 1), :].rearrange("(p j) n -> p (j n)", j=4))
-            for piece in range(2):
-                w_pieces[c, b, piece] = loaded.rearrange("p (j n) -> p j n", j=4)[:, :, PIECE * piece : PIECE * (piece + 1)]
+            w_pieces[c, b, 0] = loaded.rearrange("p (j n) -> p j n", j=4)[:, :, 0 : SCALAR_COLUMNS[i]]
+            w_pieces[c, b, 1] = loaded.rearrange("p (j n) -> p j n", j=4)[:, :, SCALAR_COLUMNS[i] : N]
 
         w1_dealt = [keep.tile([P, 2 * H], U8, name=f"w1_dealt{b}", align_bytes=64) for b in range(2)]
-        warm_bank = psum.tile([P, PASS], F32, name=f"bank{BANKS - 2}")
-        w1_bytes = w1_raw[:].bitcast(U8)
-        for i in range(2):
-            nc.tensor.matmul_mx(
-                out=warm_bank[:],
-                lhsT=w1_bytes[:, 0 : 2 * P].bitcast(FP4X4),
-                lhsT_scale=w1_scale_rows[:, 0:P],
-                rhs=w1_bytes[:, 0 : 2 * PASS].bitcast(FP4X4),
-                rhs_scale=w1_scale_rows[:, 0:PASS],
-                start=True,
-                stop=True,
-            )
         states = []
 
         def part(parted, picked_words, first, count):
@@ -156,11 +145,10 @@ def tile_list_replay_twin_critics_kernel(tc, tab, offs, w1_words, w1_scales, gai
         h_planes = [keep.tile([P, 2 * QUART], U8, name=f"h_planes{pair}", align_bytes=64) for pair in range(4)]
 
         def prepare_w(c, b):
-            for piece, copy in enumerate((nc.scalar.copy, nc.vector.tensor_copy)):
-                copy(
-                    w_grouped[c, b][:, 4 * PIECE * piece : 4 * PIECE * (piece + 1)].rearrange("p (o i j) -> p o j i", i=4, j=4),
-                    w_pieces[c, b, piece].rearrange("p j (o i) -> p o j i", i=4),
-                )
+            split = w_pieces[c, b, 0].shape[2]
+            grouped = w_grouped[c, b][:].rearrange("p (o i j) -> p o j i", i=4, j=4)
+            nc.scalar.copy(grouped[:, 0 : split // 4], w_pieces[c, b, 0].rearrange("p j (o i) -> p o j i", i=4))
+            nc.vector.tensor_copy(grouped[:, split // 4 :], w_pieces[c, b, 1].rearrange("p j (o i) -> p o j i", i=4))
             nc.vector.quantize_mx(out=w_codes[c, b][:].bitcast(FP8X4), scales=w_planes[c, b][:], in_=w_grouped[c, b][:])
 
         banks_taken = []

@@ -64,7 +64,7 @@ def tile_list_replay_twin_critics_kernel(tc, tab, offs, w1_words, w1_scales, gai
         nc.scalar.dma_start(bias_rows[P - 4 : P, :], bb.rearrange("(m p) -> m p", p=P))
         nc.vector.memset(gain_rows[0 : P - 2, :], 0.0)
         nc.vector.memset(bias_rows[0 : P - 8, :], 0.0)
-        planes = keep.tile([P, 2 * (S + H)], U8, name="planes", align_bytes=64)
+        planes = keep.tile([P, 2 * (S + H)], U8, name="planes", align_bytes=256)
         nc.gpsimd.memset(planes[:].bitcast(I32), 0)
         ident = keep.tile([P, P], F32, name="ident")
         make_identity(nc, ident[:])
@@ -104,7 +104,7 @@ def tile_list_replay_twin_critics_kernel(tc, tab, offs, w1_words, w1_scales, gai
             w_pieces[c, b, 0] = loaded.rearrange("p (j n) -> p j n", j=4)[:, :, 0 : SCALAR_COLUMNS[i]]
             w_pieces[c, b, 1] = loaded.rearrange("p (j n) -> p j n", j=4)[:, :, SCALAR_COLUMNS[i] : N]
 
-        w1_dealt = [keep.tile([P, 2 * H], U8, name=f"w1_dealt{b}", align_bytes=64) for b in range(2)]
+        w1_dealt = [keep.tile([P, 2 * H], U8, name=f"w1_dealt{b}", align_bytes=256) for b in range(2)]
         states = []
 
         def part(parted, picked_words, first, count):
@@ -124,7 +124,7 @@ def tile_list_replay_twin_critics_kernel(tc, tab, offs, w1_words, w1_scales, gai
             picked_words = keep.tile([P, HALF], U32, name="picked_words", align_bytes=64)
             list_columns = slice(s * HALF // 16, (s + 1) * HALF // 16)
             nc.vector.tensor_copy(picked_words[:], tab_words[:].bitcast(U32).indirect(offsets[:, list_columns]))
-            parted = keep.tile([P, 2 * 2 * HALF], U8, name=f"parted{s}", align_bytes=64)
+            parted = keep.tile([P, 2 * 2 * HALF], U8, name=f"parted{s}", align_bytes=256)
             if s == 0:
                 deal(0, slice(0, 2))
                 part(parted, picked_words, 0, QUART)
@@ -139,10 +139,10 @@ def tile_list_replay_twin_critics_kernel(tc, tab, offs, w1_words, w1_scales, gai
         for c in range(2):
             for b in range(2):
                 w_grouped[c, b] = keep.tile([P, 4 * N], BF16, name=f"w_grouped{c}{b}", align_bytes=64)
-                w_codes[c, b] = keep.tile([P, N], U32, name=f"w_codes{c}{b}", align_bytes=64)
-                w_planes[c, b] = keep.tile([P, N], U8, name=f"w_planes{c}{b}", align_bytes=64)
-        h_codes = [keep.tile([P, 2 * QUART], U32, name=f"h_codes{pair}", align_bytes=64) for pair in range(4)]
-        h_planes = [keep.tile([P, 2 * QUART], U8, name=f"h_planes{pair}", align_bytes=64) for pair in range(4)]
+                w_codes[c, b] = keep.tile([P, N], U32, name=f"w_codes{c}{b}", align_bytes=256)
+                w_planes[c, b] = keep.tile([P, N], U8, name=f"w_planes{c}{b}", align_bytes=256)
+        h_codes = [keep.tile([P, 2 * QUART], U32, name=f"h_codes{pair}", align_bytes=256) for pair in range(4)]
+        h_planes = [keep.tile([P, 2 * QUART], U8, name=f"h_planes{pair}", align_bytes=256) for pair in range(4)]
 
         def prepare_w(c, b):
             split = w_pieces[c, b, 0].shape[2]

@@ -86,7 +86,7 @@ def tile_list_replay_twin_critics_kernel(tc, tab, offs, w1_words, w1_scales, gai
         picked_scales = reused.tile([P, S], U8, name="picked_scales", offset=TANH_BYTES - S // 2)
         nc.vector.tensor_copy(picked_scales[:], tab_scales[:].indirect(offsets[:]))
         nc.vector.tensor_copy(scale_rows[:, 0:S].bitcast(I32), picked_scales[:].bitcast(I32))
-        for z in range(4):
+        for z in (0, 2, 1, 3):
             nc.sync.dma_start(
                 planes[32 * z : 32 * z + 4, :].bitcast(I32).rearrange("p (a x) -> p a x", a=2),
                 scale_rows[ROW0 + 8 * z : ROW0 + 8 * z + 8, :].bitcast(I32),
@@ -114,8 +114,8 @@ def tile_list_replay_twin_critics_kernel(tc, tab, offs, w1_words, w1_scales, gai
                 picked_words[:].bitcast(U16).rearrange("p (o i a) -> p o a i", a=2, i=8)[:, groups],
             )
 
-        def deal(b, slots):
-            nc.vector.tensor_copy(
+        def deal(copy, b, slots):
+            copy(
                 w1_dealt[b][:].bitcast(U16).rearrange("p (a t o i) -> p a o t i", a=2, t=4, i=8)[:, :, :, slots],
                 w1_raw[:].bitcast(U16).rearrange("p (a b o i t) -> p b a o t i", a=2, b=2, t=4, i=8)[:, b, :, :, slots],
             )
@@ -126,11 +126,11 @@ def tile_list_replay_twin_critics_kernel(tc, tab, offs, w1_words, w1_scales, gai
             nc.vector.tensor_copy(picked_words[:], tab_words[:].bitcast(U32).indirect(offsets[:, list_columns]))
             parted = keep.tile([P, 2 * 2 * HALF], U8, name=f"parted{s}", align_bytes=256)
             if s == 0:
-                deal(0, slice(0, 2))
+                deal(nc.scalar.copy, 0, slice(0, 2))
                 part(parted, picked_words, 0, QUART)
-                deal(0, slice(2, 4))
+                deal(nc.scalar.copy, 0, slice(2, 4))
                 part(parted, picked_words, QUART, QUART)
-                deal(1, slice(0, 4))
+                deal(nc.vector.tensor_copy, 1, slice(0, 4))
             else:
                 part(parted, picked_words, 0, HALF)
             states.append(parted)
@@ -211,8 +211,8 @@ def tile_list_replay_twin_critics_kernel(tc, tab, offs, w1_words, w1_scales, gai
         def h_operand(tiles, g, b):
             return tiles[b][:] if g == 0 else tiles[g + 1][:, b * QUART : (b + 1) * QUART]
 
-        def critic_sums(c, g, m0):
-            bank = next_bank()[:].rearrange("p (i n) -> p i n", n=GROUPS[g][1])
+        def critic_sums(c, g, m0, tiles=None):
+            bank = next_bank()[:].rearrange("p (i n) -> p i n", n=GROUPS[g][1])[:, 0:tiles]
             for i in range(bank.shape[1]):
                 actions = slice((m0 + i) * P, (m0 + i + 1) * P)
                 for b in (1, 0):
@@ -234,18 +234,22 @@ def tile_list_replay_twin_critics_kernel(tc, tab, offs, w1_words, w1_scales, gai
                 nc.scalar.activation(qa_tiles[g, m0][:, i, :], bank[:, i, :], ACT.Identity, bias=biases[:, m0 + i : m0 + i + 1])
 
         def critic_b(g, m0):
+            if g == len(GROUPS) - 1 and m0 + 2 == N // P:
+                for i in range(2):
+                    bank = critic_sums(1, g, m0 + i, 1)
+                    result = keep.tile([P, QUART], F32, name=f"result{g}{m0 + i}")
+                    bias_b = biases[:, 4 + m0 + i : 4 + m0 + i + 1]
+                    nc.vector.scalar_tensor_tensor(result[:], bank[:, 0, :], bias_b, qa_tiles[g, m0][:, i, :], ALU.add, ALU.min)
+                    nc.sync.dma_start(out[(m0 + i) * P : (m0 + i + 1) * P, GROUPS[g][0] : S], result[:])
+                return
             bank = critic_sums(1, g, m0)
             tiles = bank.shape[1]
             tokens = slice(GROUPS[g][0], GROUPS[g][0] + GROUPS[g][1])
             result = keep.tile(list(bank.shape), F32, name=f"result{g}{m0}")
-            last = g == len(GROUPS) - 1 and m0 + tiles == N // P
             for i in range(tiles):
                 bias_b = biases[:, 4 + m0 + i : 4 + m0 + i + 1]
                 nc.vector.scalar_tensor_tensor(result[:, i, :], bank[:, i, :], bias_b, qa_tiles[g, m0][:, i, :], ALU.add, ALU.min)
-                if last:
-                    nc.sync.dma_start(out[(m0 + i) * P : (m0 + i + 1) * P, tokens], result[:, i, :])
-            if not last:
-                nc.sync.dma_start(out.rearrange("(m p) j -> p m j", p=P)[:, m0 : m0 + tiles, tokens], result[:])
+            nc.sync.dma_start(out.rearrange("(m p) j -> p m j", p=P)[:, m0 : m0 + tiles, tokens], result[:])
 
         for b in range(2):
             prepare_w(0, b)
@@ -259,8 +263,9 @@ def tile_list_replay_twin_critics_kernel(tc, tab, offs, w1_words, w1_scales, gai
             encode(i)
         for m in range(N // P):
             critic_a(0, m)
+        for i in range(4, len(UNITS)):
+            make_h(i)
         for m in range(N // P):
-            make_h(4 + m)
             critic_b(0, m)
         for g in range(1, len(GROUPS)):
             for m0 in (0, 2):

@@ -27,7 +27,7 @@ ROW0 = 96
 BANKS = 7
 UNITS = ((0, 0), (1, 0), (0, 1), (1, 1), (2, 0), (2, 1), (3, 0), (3, 1))
 GROUPS = ((0, HALF), (2 * QUART, QUART), (3 * QUART, QUART))
-GPSIMD_TOKENS = (80, 112)
+GPSIMD_TOKENS = (64, 96)
 TANH_BYTES = len(UNITS) * 4 * QUART * 4
 
 

@@ -27,7 +27,7 @@ ROW0 = 96
 BANKS = 7
 UNITS = ((0, 0), (1, 0), (0, 1), (1, 1), (2, 0), (2, 1), (3, 0), (3, 1))
 GROUPS = ((0, HALF), (2 * QUART, QUART), (3 * QUART, QUART))
-GPSIMD_TOKENS = (64, 96)
+GPSIMD_TOKENS = (64, 72)
 TANH_BYTES = len(UNITS) * 4 * QUART * 4
 
 

@@ -22,12 +22,12 @@ PASS = 512
 HALF = S // 2
 QUART = S // 4
 PIECE = N // 2
-SCALAR_COLUMNS = (128, 256, 256)
+SCALAR_COLUMNS = (128, 320, 256)
 ROW0 = 96
 BANKS = 7
 UNITS = ((0, 0), (1, 0), (0, 1), (1, 1), (2, 0), (2, 1), (3, 0), (3, 1))
 GROUPS = ((0, HALF), (2 * QUART, QUART), (3 * QUART, QUART))
-GPSIMD_TOKENS = (64, 72)
+GPSIMD_TOKENS = (80, 76)
 TANH_BYTES = len(UNITS) * 4 * QUART * 4
 
 
@@ -130,7 +130,7 @@ def tile_list_replay_twin_critics_kernel(tc, tab, offs, w1_words, w1_scales, gai
                 part(parted, picked_words, 0, QUART)
                 deal(nc.scalar.copy, 0, slice(2, 4))
                 part(parted, picked_words, QUART, QUART)
-                deal(nc.vector.tensor_copy, 1, slice(0, 4))
+                deal(nc.scalar.copy, 1, slice(0, 4))
             else:
                 part(parted, picked_words, 0, HALF)
             states.append(parted)

from contextlib import ExitStack

import concourse.mybir as mybir
from concourse.masks import make_identity

K, T, S, H, N = 1024, 4096, 1024, 1024, 512
FLOPS = 2 * K * H * S + 2 * 2 * H * N * S

F32 = mybir.dt.float32
BF16 = mybir.dt.bfloat16
I32 = mybir.dt.int32
U32 = mybir.dt.uint32
U16 = mybir.dt.uint16
U8 = mybir.dt.uint8
FP8X4 = mybir.dt.float8_e4m3fn_x4
FP4X4 = mybir.dt.float4_e2m1fn_x4
ACT = mybir.ActivationFunctionType
ALU = mybir.AluOpType

P = 128
PASS = 512
HALF = S // 2
QUART = S // 4
PIECE = N // 2
SCALAR_COLUMNS = (128, 320, 256)
ROW0 = 96
BANKS = 7
UNITS = ((0, 0), (1, 0), (0, 1), (1, 1), (2, 0), (2, 1), (3, 0), (3, 1))
GROUPS = ((0, HALF), (2 * QUART, QUART), (3 * QUART, QUART))
GPSIMD_TOKENS = (80, 76)
TANH_BYTES = len(UNITS) * 4 * QUART * 4


def tile_list_replay_twin_critics_kernel(tc, tab, offs, w1_words, w1_scales, gain, wa, ba, wb, bb, out):
    nc = tc.nc
    with ExitStack() as ctx:
        keep = ctx.enter_context(tc.tile_pool(name="keep", bufs=1))
        ring = ctx.enter_context(tc.tile_pool(name="ring", bufs=2))
        reused = ctx.enter_context(tc.tile_pool(name="reused", bufs=1))
        psum = ctx.enter_context(tc.psum_pool(name="psum", bufs=1))

        offsets = keep.tile([P, S // 16], U16, name="offsets")
        nc.sync.dma_start(offsets[:], offs)

        tab_scales = keep.tile([P, T], U8, name="tab_scales", align_bytes=64)
        w1_scale_rows = keep.tile([P, H], U8, name="w1_scale_rows", align_bytes=64)
        nc.sync.dma_start(
            tab_scales[ROW0:P, :].bitcast(I32),
            tab[0:1, PASS * T :].rearrange("o (a g t) -> (o g) a t", a=2, g=16).bitcast(I32),
        )
        nc.sync.dma_start(w1_scale_rows[ROW0:P, :].bitcast(I32), w1_scales.rearrange("a g c -> g a c").bitcast(I32))
        tab_words = keep.tile([P, T], I32, name="tab_words", align_bytes=64)
        nc.sync.dma_start(tab_words[:], tab[0:1, 0 : PASS * T].rearrange("o (p x) -> (o p) x", p=P).bitcast(I32))
        w1_raw = keep.tile([P, H], I32, name="w1_raw", align_bytes=64)
        nc.sync.dma_start(w1_raw[:].rearrange("p (a x) -> p a x", a=2), w1_words.rearrange("a p x -> p a x").bitcast(I32))

        nc.vector.memset(w1_scale_rows[0:ROW0, :].bitcast(I32), 0)
        nc.vector.memset(tab_scales[0:ROW0, :].bitcast(I32), 0)

        gain_rows = keep.tile([P, PASS], F32, name="gain_rows")
        bias_rows = keep.tile([P, P], F32, name="bias_rows")
        nc.scalar.dma_start(gain_rows[P - 2 : P, :], gain.rearrange("(b x) -> b x", b=2))
        nc.scalar.dma_start(bias_rows[P - 8 : P - 4, :], ba.rearrange("(m p) -> m p", p=P))
        nc.scalar.dma_start(bias_rows[P - 4 : P, :], bb.rearrange("(m p) -> m p", p=P))
        nc.vector.memset(gain_rows[0 : P - 2, :], 0.0)
        nc.vector.memset(bias_rows[0 : P - 8, :], 0.0)
        planes = keep.tile([P, 2 * (S + H)], U8, name="planes", align_bytes=256)
        nc.gpsimd.memset(planes[:].bitcast(I32), 0)
        ident = keep.tile([P, P], F32, name="ident")
        make_identity(nc, ident[:])
        gain_bank = psum.tile([P, 4, P], F32, name="gain_bank")
        for t in range(4):
            nc.tensor.transpose(gain_bank[:, t, :], gain_rows[:, t:PASS:4], ident[:])
        gain_sbuf = keep.tile([P, 2, 4], F32, name="gain_sbuf")
        nc.scalar.activation(gain_sbuf[:], gain_bank[:, :, P - 2 : P].rearrange("p t b -> p b t"), ACT.Copy)
        bias_bank = psum.tile([P, P], F32, name=f"bank{BANKS - 1}")
        nc.tensor.transpose(bias_bank[:], bias_rows[:], ident[:])
        biases = keep.tile([P, 8], F32, name="biases")
        nc.scalar.activation(biases[:], bias_bank[:, P - 8 : P], ACT.Copy)

        scale_rows = keep.tile([P, S + H], U8, name="scale_rows", align_bytes=64)
        nc.vector.tensor_copy(
            scale_rows[:, S:].rearrange("p (b t o i) -> p b o t i", b=2, t=4, i=16),
            w1_scale_rows[:].rearrange("p (b o i t) -> p b o t i", b=2, t=4, i=16),
        )
        picked_scales = reused.tile([P, S], U8, name="picked_scales", offset=TANH_BYTES - S // 2)
        nc.vector.tensor_copy(picked_scales[:], tab_scales[:].indirect(offsets[:]))
        nc.vector.tensor_copy(scale_rows[:, 0:S].bitcast(I32), picked_scales[:].bitcast(I32))
        for z in (0, 2, 1, 3):
            nc.sync.dma_start(
                planes[32 * z : 32 * z + 4, :].bitcast(I32).rearrange("p (a x) -> p a x", a=2),
                scale_rows[ROW0 + 8 * z : ROW0 + 8 * z + 8, :].bitcast(I32),
            )

        wa_first = reused.tile([P, 4, PIECE], F32, name="wa_first", offset=TANH_BYTES - 4 * PIECE * 4)
        nc.sync.dma_start(wa_first[:], wa[0:PASS, 0:PIECE].rearrange("(p j) n -> p j n", j=4))
        w_rest = reused.tile([P, 4 * PIECE + 3 * 4 * N], F32, name="w_rest", offset=TANH_BYTES)
        wa_second = w_rest[:, 0 : 4 * PIECE].rearrange("p (j n) -> p j n", j=4)
        nc.sync.dma_start(wa_second, wa[0:PASS, PIECE:N].rearrange("(p j) n -> p j n", j=4))
        w_pieces = {(0, 0, 0): wa_first[:], (0, 0, 1): wa_second}
        for i, (c, b) in enumerate(((0, 1), (1, 0), (1, 1))):
            loaded = w_rest[:, 4 * PIECE + 4 * N * i : 4 * PIECE + 4 * N * (i + 1)]
            nc.sync.dma_start(loaded, (wa, wb)[c][PASS * b : PASS * (b + 1), :].rearrange("(p j) n -> p (j n)", j=4))
            w_pieces[c, b, 0] = loaded.rearrange("p (j n) -> p j n", j=4)[:, :, 0 : SCALAR_COLUMNS[i]]
            w_pieces[c, b, 1] = loaded.rearrange("p (j n) -> p j n", j=4)[:, :, SCALAR_COLUMNS[i] : N]

        w1_dealt = [keep.tile([P, 2 * H], U8, name=f"w1_dealt{b}", align_bytes=256) for b in range(2)]
        states = []

        def part(parted, picked_words, first, count):
            groups = slice(first // 8, (first + count) // 8)
            nc.vector.tensor_copy(
                parted[:].bitcast(U16).rearrange("p (a o i) -> p o a i", a=2, i=8)[:, groups],
                picked_words[:].bitcast(U16).rearrange("p (o i a) -> p o a i", a=2, i=8)[:, groups],
            )

        def deal(copy, b, slots):
            copy(
                w1_dealt[b][:].bitcast(U16).rearrange("p (a t o i) -> p a o t i", a=2, t=4, i=8)[:, :, :, slots],
                w1_raw[:].bitcast(U16).rearrange("p (a b o i t) -> p b a o t i", a=2, b=2, t=4, i=8)[:, b, :, :, slots],
            )

        for s in range(2):
            picked_words = keep.tile([P, HALF], U32, name="picked_words", align_bytes=64)
            list_columns = slice(s * HALF // 16, (s + 1) * HALF // 16)
            nc.vector.tensor_copy(picked_words[:], tab_words[:].bitcast(U32).indirect(offsets[:, list_columns]))
            parted = keep.tile([P, 2 * 2 * HALF], U8, name=f"parted{s}", align_bytes=256)
            if s == 0:
                deal(nc.scalar.copy, 0, slice(0, 2))
                part(parted, picked_words, 0, QUART)
                deal(nc.scalar.copy, 0, slice(2, 4))
                part(parted, picked_words, QUART, QUART)
                deal(nc.scalar.copy, 1, slice(0, 4))
            else:
                part(parted, picked_words, 0, HALF)
            states.append(parted)

        w_grouped, w_codes, w_planes = {}, {}, {}
        for c in range(2):
            for b in range(2):
                w_grouped[c, b] = keep.tile([P, 4 * N], BF16, name=f"w_grouped{c}{b}", align_bytes=64)
                w_codes[c, b] = keep.tile([P, N], U32, name=f"w_codes{c}{b}", align_bytes=256)
                w_planes[c, b] = keep.tile([P, N], U8, name=f"w_planes{c}{b}", align_bytes=256)
        h_codes = [keep.tile([P, 2 * QUART], U32, name=f"h_codes{pair}", align_bytes=256) for pair in range(4)]
        h_planes = [keep.tile([P, 2 * QUART], U8, name=f"h_planes{pair}", align_bytes=256) for pair in range(4)]

        def prepare_w(c, b):
            split = w_pieces[c, b, 0].shape[2]
            grouped = w_grouped[c, b][:].rearrange("p (o i j) -> p o j i", i=4, j=4)
            nc.scalar.copy(grouped[:, 0 : split // 4], w_pieces[c, b, 0].rearrange("p j (o i) -> p o j i", i=4))
            nc.vector.tensor_copy(grouped[:, split // 4 :], w_pieces[c, b, 1].rearrange("p j (o i) -> p o j i", i=4))
            nc.vector.quantize_mx(out=w_codes[c, b][:].bitcast(FP8X4), scales=w_planes[c, b][:], in_=w_grouped[c, b][:])

        banks_taken = []

        def next_bank():
            banks_taken.append(psum.tile([P, 2 * QUART], F32, name=f"bank{len(banks_taken) % BANKS}"))
            return banks_taken[-1]

        tanh_values = reused.tile([P, len(UNITS) * 4 * QUART], F32, name="tanh_values", offset=0)
        h_grouped, qa_tiles = {}, {}

        def tanh_of(i):
            return tanh_values[:, 4 * QUART * i : 4 * QUART * (i + 1)].rearrange("p (u n v) -> p u n v", u=2, v=2)

        def encode(i):
            q, b = UNITS[i]
            s, j0 = divmod(q * QUART, HALF)
            for u in range(2):
                bank = next_bank()
                for v in range(2):
                    t = 2 * u + v
                    for a in range(2):
                        w1_col = a * PASS + t * P
                        state_col = a * HALF + j0
                        plane = planes[:, a * (S + H) : (a + 1) * (S + H)]
                        nc.tensor.matmul_mx(
                            out=bank[:, v * QUART : (v + 1) * QUART],
                            lhsT=w1_dealt[b][:, 2 * w1_col : 2 * (w1_col + P)].bitcast(FP4X4),
                            lhsT_scale=plane[:, S + b * PASS + t * P : S + b * PASS + (t + 1) * P],
                            rhs=states[s][:, 2 * state_col : 2 * (state_col + QUART)].bitcast(FP4X4),
                            rhs_scale=plane[:, q * QUART : (q + 1) * QUART],
                            start=(a == 0),
                            stop=(a == 1),
                        )
                nc.scalar.activation(tanh_of(i)[:, u], bank[:].rearrange("p (v n) -> p n v", v=2), ACT.Tanh)

        def make_h(i):
            b = UNITS[i][1]
            pair, side = divmod(i, 2)
            if side == 0:
                h_grouped[pair] = ring.tile([P, 2 * 4 * QUART], BF16, name="h_grouped", align_bytes=64)
            grouped = h_grouped[pair][:, 4 * QUART * side : 4 * QUART * (side + 1)].rearrange("p (n u v) -> p n u v", u=2, v=2)
            split = QUART - GPSIMD_TOKENS[i // 4]
            values = tanh_of(i).rearrange("p u n v -> p n u v")
            nc.vector.tensor_tensor(
                grouped[:, 0:split],
                values[:, 0:split],
                gain_bank[:, :, P - 2 + b : P - 1 + b].rearrange("p (u v) o -> p o u v", u=2).to_broadcast([P, split, 2, 2]),
                ALU.mult,
            )
            nc.gpsimd.tensor_tensor(
                grouped[:, split:],
                values[:, split:],
                gain_sbuf[:, b : b + 1, :].rearrange("p o (u v) -> p o u v", u=2).to_broadcast([P, QUART - split, 2, 2]),
                ALU.mult,
            )
            if side == 1:
                nc.vector.quantize_mx(out=h_codes[pair][:].bitcast(FP8X4), scales=h_planes[pair][:], in_=h_grouped[pair][:])

        def h_operand(tiles, g, b):
            return tiles[b][:] if g == 0 else tiles[g + 1][:, b * QUART : (b + 1) * QUART]

        def critic_sums(c, g, m0, tiles=None):
            bank = next_bank()[:].rearrange("p (i n) -> p i n", n=GROUPS[g][1])[:, 0:tiles]
            for i in range(bank.shape[1]):
                actions = slice((m0 + i) * P, (m0 + i + 1) * P)
                for b in (1, 0):
                    nc.tensor.matmul_mx(
                        out=bank[:, i, :],
                        lhsT=w_codes[c, b][:, actions].bitcast(FP8X4),
                        lhsT_scale=w_planes[c, b][:, actions],
                        rhs=h_operand(h_codes, g, b).bitcast(FP8X4),
                        rhs_scale=h_operand(h_planes, g, b),
                        start=(b == 1),
                        stop=(b == 0),
                    )
            return bank

        def critic_a(g, m0):
            bank = critic_sums(0, g, m0)
            qa_tiles[g, m0] = keep.tile(list(bank.shape), F32, name=f"qa{g}{m0}")
            for i in range(bank.shape[1]):
                nc.scalar.activation(qa_tiles[g, m0][:, i, :], bank[:, i, :], ACT.Identity, bias=biases[:, m0 + i : m0 + i + 1])

        def critic_b(g, m0):
            if g == len(GROUPS) - 1 and m0 + 2 == N // P:
                for i in range(2):
                    bank = critic_sums(1, g, m0 + i, 1)
                    result = keep.tile([P, QUART], F32, name=f"result{g}{m0 + i}")
                    bias_b = biases[:, 4 + m0 + i : 4 + m0 + i + 1]
                    nc.vector.scalar_tensor_tensor(result[:], bank[:, 0, :], bias_b, qa_tiles[g, m0][:, i, :], ALU.add, ALU.min)
                    nc.sync.dma_start(out[(m0 + i) * P : (m0 + i + 1) * P, GROUPS[g][0] : S], result[:])
                return
            bank = critic_sums(1, g, m0)
            tiles = bank.shape[1]
            tokens = slice(GROUPS[g][0], GROUPS[g][0] + GROUPS[g][1])
            result = keep.tile(list(bank.shape), F32, name=f"result{g}{m0}")
            for i in range(tiles):
                bias_b = biases[:, 4 + m0 + i : 4 + m0 + i + 1]
                nc.vector.scalar_tensor_tensor(result[:, i, :], bank[:, i, :], bias_b, qa_tiles[g, m0][:, i, :], ALU.add, ALU.min)
            nc.sync.dma_start(out.rearrange("(m p) j -> p m j", p=P)[:, m0 : m0 + tiles, tokens], result[:])

        for b in range(2):
            prepare_w(0, b)
        for i in range(4):
            encode(i)
            make_h(i)
        for b in range(2):
            prepare_w(1, b)
            encode(4 + b)
        for i in range(6, len(UNITS)):
            encode(i)
        for m in range(N // P):
            critic_a(0, m)
        for i in range(4, len(UNITS)):
            make_h(i)
        for m in range(N // P):
            critic_b(0, m)
        for g in range(1, len(GROUPS)):
            for m0 in (0, 2):
                critic_a(g, m0)
                critic_b(g, m0)
